import numpy as np
import ml_dtypes


def mxq(x, axis, fmt="e4m3"):
    dtype, down = {"e4m3": (ml_dtypes.float8_e4m3fn, 7), "e5m2": (ml_dtypes.float8_e5m2, 14)}[fmt]
    v = np.moveaxis(np.asarray(x, np.float32).astype(ml_dtypes.bfloat16).astype(np.float64), axis, -1)
    blocks = v.reshape(v.shape[:-1] + (-1, 32))
    amax = np.abs(blocks).max(-1, keepdims=True)
    byte = np.maximum(np.where(amax > 0, np.frexp(amax)[1] - 1 + 127, 0) - down, 1)
    scale = np.exp2(byte - 127.0)
    codes = (blocks / scale).astype(np.float32).astype(dtype).astype(np.float64)
    return np.moveaxis((codes * scale).reshape(v.shape), -1, axis)


WIDE = False


def mx_kscale(k):
    if not WIDE:
        return np.ones(k)
    levels = np.array([10, -10, 5, -5, 0])
    if k % 512:
        return np.exp2(np.random.permutation(np.resize(levels, k // 32))).repeat(32)
    a = np.empty((k // 512, 16))
    for p in range(k // 512):
        a[p, :8] = np.random.permutation(np.resize(levels, 8))
        for g in range(8):
            far = levels[np.abs(levels - a[p, g]) >= 10]
            a[p, g + 8] = far[np.random.randint(len(far))]
    return np.exp2(a.ravel()).repeat(32)


def f64(x):
    return np.asarray(x).astype(np.float64)


def striped(idx):
    return np.tile(idx.reshape(-1, 16).T, (8, 1)).astype(np.uint16)


def unstriped(offs):
    return offs[:16].T.reshape(-1).astype(np.int64)


def sigmoid(v):
    return 1.0 / (1.0 + np.exp(-np.maximum(v, -700.0)))


K, T, E, C, H, N = 2560, 512, 2, 256, 512, 256


def by_expert(wq, xq):
    return np.concatenate([wq[e].T @ xq[:, e * C:(e + 1) * C] for e in range(E)], axis=1)


def setup_inputs():
    n = np.random.standard_normal
    s = mx_kscale(K)[:, None]
    u = mx_kscale(H)
    return {
        "xT": (n((K, T)) * s).astype(np.float32),
        "w1": (n((E, K, H)) / np.sqrt(K) / s[None]).astype(np.float32),
        "w3": (n((E, K, H)) / np.sqrt(K) / s[None] * u[None, None, :]).astype(np.float32),
        "w2": (n((E, H, N)) / np.sqrt(H) / u[None, :, None]).astype(np.float32),
        "gate": np.tile(np.random.uniform(0.2, 1.0, E * C), (N, 1)).astype(np.float32),
        "offs": striped(np.random.permutation(T)[:E * C]),
        "dst": striped(np.random.permutation(T)[:E * C]),
    }


def reference(xT, w1, w3, w2, gate, offs, dst):
    idx = unstriped(offs)
    xq = mxq(f64(xT)[:, idx], 0, "e4m3")
    h = sigmoid(by_expert(mxq(f64(w1), 1, "e4m3"), xq))
    h = h * by_expert(mxq(f64(w3), 1, "e4m3"), xq)
    y = by_expert(mxq(f64(w2), 1, "e4m3"), mxq(h, 0, "e4m3"))
    out = np.zeros((N, T))
    out[:, unstriped(dst)] = f64(gate) * y
    return out

@@ -1,0 +1,274 @@
+from contextlib import ExitStack
+
+import concourse.mybir as mybir
+
+K, T, E, C, H, N = 2560, 512, 2, 256, 512, 256
+P = 128
+PACK = 4
+K_PASS = P * PACK
+PASSES = K // K_PASS
+FLOPS = 2 * E * C * (2 * K * H + H * N)
+
+F32 = mybir.dt.float32
+BF16 = mybir.dt.bfloat16
+U32 = mybir.dt.uint32
+U16 = mybir.dt.uint16
+U8 = mybir.dt.uint8
+FP8X4 = mybir.dt.float8_e4m3fn_x4
+SIGMOID = mybir.ActivationFunctionType.Sigmoid
+MULT = mybir.AluOpType.mult
+
+VECTOR_SHARE = {("x", 0): 40, ("w1", 0): 40, ("w3", 0): 44, ("w2", 0): 40, ("w1", 1): 40, ("w3", 1): 64, ("w2", 1): 0}
+
+
+def tile_moe_two_glu_sigmoid_kernel(tc, xT, w1, w3, w2, gate, offs, dst, out):
+    nc = tc.nc
+    with ExitStack() as ctx:
+        lists = ctx.enter_context(tc.tile_pool(name="lists", bufs=1))
+        keep = ctx.enter_context(tc.tile_pool(name="keep", bufs=1))
+        stage = ctx.enter_context(tc.tile_pool(name="stage", bufs=8))
+        work = ctx.enter_context(tc.tile_pool(name="work", bufs=4))
+        psum = ctx.enter_context(tc.psum_pool(name="psum", bufs=1))
+
+        offs_sb = lists.tile([P, E * C // 16], U16, name="offs_sb")
+        dst_sb = lists.tile([P, E * C // 16], U16, name="dst_sb")
+
+        warm_in = keep.tile([P, 1], F32, name="warm_in")
+        warm_out = keep.tile([P, 1], F32, name="warm_out")
+        nc.vector.memset(warm_in[:], 0.0)
+        nc.scalar.activation(warm_out[:], warm_in[:], SIGMOID)
+
+        bytes_all = [keep.tile([P, T], U8, name=f"bytes_all{g}", align_bytes=64) for g in range(2)]
+        bytes_slot = [keep.tile([P, E * C], U8, name=f"bytes_slot{g}", align_bytes=64) for g in range(2)]
+        for b in bytes_all:
+            nc.gpsimd.memset(b[:], 0)
+        words_all = [keep.tile([P, T], U32, name=f"words_all{s}", align_bytes=64) for s in range(PASSES)]
+        words_slot = [keep.tile([P, E * C], U32, name=f"words_slot{s}", align_bytes=64) for s in range(PASSES)]
+        gate_sb = [keep.tile([P, 2, C], F32, name=f"gate_sb{e}") for e in range(E)]
+        placed = [keep.tile([P, T], F32, name=f"placed{q}") for q in range(N // P)]
+
+        def load(rows):
+            count, width = rows.shape[0] // K_PASS, rows.shape[1]
+            raw = stage.tile([P, count, PACK, width], F32, name=f"raw{count}_{width}", bufs={(2, 512): 4, (1, 512): 8, (1, 256): 2}[count, width])
+            nc.sync.dma_start(raw[:], rows.rearrange("(a p j) w -> p a j w", p=P, j=PACK))
+            return [raw[:, a] for a in range(count)]
+
+        def load_halves(rows):
+            view = rows.rearrange("(p j) w -> p j w", j=PACK)
+            halves = []
+            for v in range(2):
+                half = stage.tile([P, 2, H], F32, name=f"half{v}", bufs=1)
+                nc.sync.dma_start(half[:], view[:, 2 * v:2 * v + 2, :])
+                halves.append(half)
+            return halves
+
+        def interleave_halves(halves):
+            grouped = work.tile([P, H * PACK], BF16, name="grouped512", align_bytes=64)
+            to = grouped[:].rearrange("p (t m i j) -> p m j t i", t=4, i=2, j=PACK)
+            fro = [half[:].rearrange("p j (m i t) -> p m j t i", t=4, i=2) for half in halves]
+            nc.scalar.copy(to[:, :, 0:2], fro[0])
+            nc.vector.tensor_copy(to[:, :, 2:4], fro[1])
+            return grouped
+
+        def interleave(raw, permute, share):
+            width = raw.shape[2]
+            grouped = work.tile([P, width * PACK], BF16, name=f"grouped{width}", align_bytes=64)
+            if permute:
+                to = grouped[:].rearrange("p (t m i j) -> p m j t i", t=4, i=2, j=PACK)
+                fro = raw.rearrange("p j (m i t) -> p m j t i", t=4, i=2)
+            else:
+                to = grouped[:].rearrange("p (c i j) -> p c j i", i=4, j=PACK)
+                fro = raw.rearrange("p j (c i) -> p c j i", i=4)
+            blocks = to.shape[1]
+            cut = blocks * share // 256 * 2
+            if cut > 0:
+                nc.vector.tensor_copy(to[:, :cut], fro[:, :cut])
+            if cut < blocks:
+                nc.scalar.copy(to[:, cut:], fro[:, cut:])
+            return grouped
+
+        def quantize(grouped, codes, scales):
+            nc.vector.quantize_mx(out=codes.bitcast(FP8X4), scales=scales, in_=grouped[:])
+
+        def x_scales(s):
+            return bytes_slot[s // 4], 4 * (s % 4)
+
+        def banks(base):
+            return [psum.tile([P, 512], F32, tag=f"bank{base + t}", name=f"acc{base + t}") for t in range(4)]
+
+        def gather_words(s, e):
+            nc.vector.tensor_copy(words_slot[s][:, e * C:(e + 1) * C], words_all[s][:].indirect(offs_sb[:, e * 16:(e + 1) * 16]))
+
+        def gather_bytes(g, e):
+            nc.vector.tensor_copy(bytes_slot[g][:, e * C:(e + 1) * C], bytes_all[g][:].indirect(offs_sb[:, e * 16:(e + 1) * 16]))
+
+        def multiply(acc, codes, scales, s, e):
+            plane, k = x_scales(s)
+            cols = slice(e * C, (e + 1) * C)
+            for t in range(4):
+                m = slice(t * P, (t + 1) * P)
+                nc.tensor.matmul_mx(
+                    out=acc[t][:, :C],
+                    lhsT=codes[:, m].bitcast(FP8X4),
+                    lhsT_scale=scales[:, m],
+                    rhs=words_slot[s][:, cols].bitcast(FP8X4),
+                    rhs_scale=plane[k:P, cols],
+                    start=(s == 0),
+                    stop=(s == PASSES - 1),
+                )
+
+        groups = [[("x", 0, 0)], [("w1", 0, 0)]]
+        for s in range(1, PASSES):
+            groups += [[("x", 0, s)], [("w1", 0, s)]]
+        for kind, e in (("w3", 0), ("w1", 1), ("w3", 1)):
+            groups += [[(kind, e, s)] for s in range(PASSES)]
+            if kind == "w3":
+                groups.append([("w2", e, 0)])
+
+        weights = {"w1": w1, "w3": w3, "w2": w2}
+        made = {}
+        acc = {}
+        sig = {}
+
+        def after(kind, e, s):
+            if kind == "x":
+                gather_words(s, 0)
+                if s == 3:
+                    gather_bytes(0, 0)
+                if s == PASSES - 1:
+                    gather_bytes(1, 0)
+                return
+            if kind == "w2":
+                return
+            if kind == "w1" and e == 0:
+                if s < PASSES - 1:
+                    return
+                acc["w1"] = banks(0)
+                for r in range(PASSES):
+                    multiply(acc["w1"], *made["w1", 0, r], r, 0)
+            else:
+                if s == 0:
+                    acc[kind] = banks(0 if kind == "w1" else 4)
+                multiply(acc[kind], *made[kind, e, s], s, e)
+            if kind == "w3" and e == 0:
+                gather_words(s, 1)
+                if s < 2:
+                    gather_bytes(s, 1)
+            if s == PASSES - 1:
+                if kind == "w1":
+                    sig[e] = keep.tile([P, 4, C], F32, name=f"sig{e}")
+                    for t in range(4):
+                        nc.scalar.activation(sig[e][:, t, :], acc["w1"][t][:, :C], SIGMOID)
+                else:
+                    hidden(e)
+
+        def parts(e):
+            return 1 if e == 0 else 2
+
+        def hidden(e):
+            n_parts = parts(e)
+            width = C // n_parts
+            made["h", e] = []
+            tiles = []
+            for u in range(n_parts):
+                cols = slice(u * width, (u + 1) * width)
+                hb = keep.tile([P, 4, width], BF16, name=f"hb{e}{u}")
+                for t in range(4):
+                    nc.vector.tensor_tensor(hb[:, t, :], acc["w3"][t][:, cols], sig[e][:, t, cols], MULT)
+                hi = keep.tile([P, width * 4], BF16, name=f"hi{e}{u}", align_bytes=64)
+                tiles.append((hb, hi))
+                if e == 1 and u == 0:
+                    g, c, sc = waiting.pop(0)[:3]
+                    quantize(g, c, sc)
+                    nc.scalar.copy(hi[:].rearrange("p (c i t) -> p c t i", i=4, t=4), hb[:].rearrange("p t (c i) -> p c t i", i=4))
+            for u in range(n_parts):
+                hb, hi = tiles[u]
+                if not (e == 1 and u == 0):
+                    nc.vector.tensor_copy(hi[:].rearrange("p (c i t) -> p c t i", i=4, t=4), hb[:].rearrange("p t (c i) -> p c t i", i=4))
+                codes = keep.tile([P, width], U32, name=f"h_codes{e}{u}", align_bytes=64)
+                scales = keep.tile([P, width], U8, name=f"h_scales{e}{u}", align_bytes=64)
+                quantize(hi, codes[:], scales[:])
+                made["h", e].append((codes, scales))
+
+        def second(e):
+            n_parts = parts(e)
+            width = C // n_parts
+            codes, scales = made["w2", e, 0]
+            for u in range(n_parts):
+                h_codes, h_scales = made["h", e][u]
+                b = (4 if e == 0 else 0) + u
+                y = psum.tile([P, 512], F32, tag=f"bank{b}", name=f"y{e}{u}")
+                for q in range(N // P):
+                    n = slice(q * P, (q + 1) * P)
+                    nc.tensor.matmul_mx(
+                        out=y[:, q * width:(q + 1) * width],
+                        lhsT=codes[:, n].bitcast(FP8X4),
+                        lhsT_scale=scales[:, n],
+                        rhs=h_codes[:].bitcast(FP8X4),
+                        rhs_scale=h_scales[:],
+                        start=True,
+                        stop=True,
+                    )
+                ysb = keep.tile([P, 2, width], F32, name=f"ysb{e}{u}")
+                nc.scalar.copy(ysb[:], y[:, :2 * width].rearrange("p (q c) -> p q c", q=2))
+                first = e * 16 + u * (width // 16)
+                for q in range(N // P):
+                    nc.vector.tensor_tensor(placed[q][:].indirect(dst_sb[:, first:first + width // 16]), ysb[:, q, :], gate_sb[e][:, q, u * width:(u + 1) * width], MULT)
+                    if e == E - 1 and u == n_parts - 1:
+                        nc.sync.dma_start(out[q * P:(q + 1) * P, :], placed[q][:])
+
+        def load_gate(e):
+            nc.sync.dma_start(gate_sb[e][:], gate[:, e * C:(e + 1) * C].rearrange("(q p) s -> p q s", p=P))
+
+        raws = {}
+        waiting = []
+
+        def load_group(i, group):
+            kind, e, s = group[0]
+            source = xT if kind == "x" else weights[kind][e]
+            rows = source[s * K_PASS:(s + len(group)) * K_PASS, :]
+            if group == [("w3", 1, PASSES - 1)]:
+                raws[group[0]] = load_halves(rows)
+            else:
+                for key, raw in zip(group, load(rows)):
+                    raws[key] = raw
+            if i == 0:
+                nc.sync.dma_start(offs_sb[:], offs)
+            if kind == "w2":
+                if e == 0:
+                    nc.sync.dma_start(dst_sb[:], dst)
+                load_gate(e)
+
+        def process(kind, e, s):
+            raw = raws[kind, e, s]
+            if (kind, e, s) == ("w3", 1, PASSES - 1):
+                grouped = interleave_halves(raw)
+            else:
+                grouped = interleave(raw, kind in ("w1", "w3"), VECTOR_SHARE[kind, e])
+            if kind == "x":
+                k = 4 * (s % 4)
+                codes, scales = words_all[s][:], bytes_all[s // 4][k:P, :]
+            else:
+                width = N if kind == "w2" else H
+                codes_t = keep.tile([P, width], U32, name=f"{kind}c{e}{s}", align_bytes=64)
+                scales_t = keep.tile([P, width], U8, name=f"{kind}s{e}{s}", align_bytes=64)
+                made[kind, e, s] = (codes_t, scales_t)
+                codes, scales = codes_t[:], scales_t[:]
+            waiting.append((grouped, codes, scales, kind, e, s))
+            if len(waiting) > 1:
+                g, c, sc, kd, ee, ss = waiting.pop(0)
+                if (kd, ee, ss) == ("w3", 1, PASSES - 1):
+                    for t in range(4):
+                        m = slice(t * P, (t + 1) * P)
+                        nc.vector.quantize_mx(out=c[:, m].bitcast(FP8X4), scales=sc[:, m], in_=g[:, t * 512:(t + 1) * 512])
+                else:
+                    quantize(g, c, sc)
+                after(kd, ee, ss)
+                if kd == "w2" and ee == 0:
+                    second(0)
+
+        for i, group in enumerate(groups):
+            load_group(i, group)
+            for key in group:
+                process(*key)
+        second(1)

@@ -1,6 +1,7 @@
 from contextlib import ExitStack
 
 import concourse.mybir as mybir
+from concourse.masks import make_identity
 
 K, T, E, C, H, N = 2560, 512, 2, 256, 512, 256
 P = 128
@@ -18,7 +19,12 @@ FP8X4 = mybir.dt.float8_e4m3fn_x4
 SIGMOID = mybir.ActivationFunctionType.Sigmoid
 MULT = mybir.AluOpType.mult
 
-VECTOR_SHARE = {("x", 0): 40, ("w1", 0): 40, ("w3", 0): 44, ("w2", 0): 40, ("w1", 1): 40, ("w3", 1): 64, ("w2", 1): 0}
+PAIRED = {}
+RUN = 4
+WHOLE = (0, H)
+GROUPS = [[(0, 256), (256, 384), (384, 512)], [WHOLE]]
+VECTOR_COLUMNS = {("x", 0): (128,) * 5, ("w1", 0): (128,) * 5, ("w3", 0): (256,) * 5, ("w2", 0): (80,) * 5, ("w1", 1): (128,) * 5, ("w3", 1): (336,) * 5, ("w2", 1): (0,) * 5}
+LAST_PIECES = [(3, (0, 256), 96), (3, (256, 512), 96), (4, (0, 256), 96), (4, (256, 384), 0), (4, (384, 512), 64)]
 
 
 def tile_moe_two_glu_sigmoid_kernel(tc, xT, w1, w3, w2, gate, offs, dst, out):
@@ -26,8 +32,8 @@ def tile_moe_two_glu_sigmoid_kernel(tc, xT, w1, w3, w2, gate, offs, dst, out):
     with ExitStack() as ctx:
         lists = ctx.enter_context(tc.tile_pool(name="lists", bufs=1))
         keep = ctx.enter_context(tc.tile_pool(name="keep", bufs=1))
-        stage = ctx.enter_context(tc.tile_pool(name="stage", bufs=8))
-        work = ctx.enter_context(tc.tile_pool(name="work", bufs=4))
+        stage = ctx.enter_context(tc.tile_pool(name="stage", bufs=1))
+        work = ctx.enter_context(tc.tile_pool(name="work", bufs=1))
         psum = ctx.enter_context(tc.psum_pool(name="psum", bufs=1))
 
         offs_sb = lists.tile([P, E * C // 16], U16, name="offs_sb")
@@ -42,59 +48,46 @@ def tile_moe_two_glu_sigmoid_kernel(tc, xT, w1, w3, w2, gate, offs, dst, out):
         bytes_slot = [keep.tile([P, E * C], U8, name=f"bytes_slot{g}", align_bytes=64) for g in range(2)]
         for b in bytes_all:
             nc.gpsimd.memset(b[:], 0)
+        identity = keep.tile([P, P], F32, name="identity")
+        make_identity(nc, identity[:])
         words_all = [keep.tile([P, T], U32, name=f"words_all{s}", align_bytes=64) for s in range(PASSES)]
         words_slot = [keep.tile([P, E * C], U32, name=f"words_slot{s}", align_bytes=64) for s in range(PASSES)]
-        gate_sb = [keep.tile([P, 2, C], F32, name=f"gate_sb{e}") for e in range(E)]
+        gate_sb = [keep.tile([P, C], F32, name=f"gate_sb{e}") for e in range(E)]
         placed = [keep.tile([P, T], F32, name=f"placed{q}") for q in range(N // P)]
 
-        def load(rows):
-            count, width = rows.shape[0] // K_PASS, rows.shape[1]
-            raw = stage.tile([P, count, PACK, width], F32, name=f"raw{count}_{width}", bufs={(2, 512): 4, (1, 512): 8, (1, 256): 2}[count, width])
+        weights = {"w1": w1, "w3": w3, "w2": w2}
+        made = {}
+        acc = {}
+        sig = {}
+        hidden = {}
+        woven = {}
+        results = {}
+        raws = {}
+
+        def load(kind, e, first, count, cols):
+            source = xT if kind == "x" else weights[kind][e]
+            rows = source[first * K_PASS:(first + count) * K_PASS, cols[0]:cols[1]]
+            width = cols[1] - cols[0]
+            raw = stage.tile([P, count, PACK, width], F32, name=f"raw{count}_{width}", bufs={(1, 512): 8, (1, 256): 5, (1, 128): 2}[count, width])
             nc.sync.dma_start(raw[:], rows.rearrange("(a p j) w -> p a j w", p=P, j=PACK))
-            return [raw[:, a] for a in range(count)]
+            return raw
 
-        def load_halves(rows):
-            view = rows.rearrange("(p j) w -> p j w", j=PACK)
-            halves = []
-            for v in range(2):
-                half = stage.tile([P, 2, H], F32, name=f"half{v}", bufs=1)
-                nc.sync.dma_start(half[:], view[:, 2 * v:2 * v + 2, :])
-                halves.append(half)
-            return halves
-
-        def interleave_halves(halves):
-            grouped = work.tile([P, H * PACK], BF16, name="grouped512", align_bytes=64)
-            to = grouped[:].rearrange("p (t m i j) -> p m j t i", t=4, i=2, j=PACK)
-            fro = [half[:].rearrange("p j (m i t) -> p m j t i", t=4, i=2) for half in halves]
-            nc.scalar.copy(to[:, :, 0:2], fro[0])
-            nc.vector.tensor_copy(to[:, :, 2:4], fro[1])
-            return grouped
-
-        def interleave(raw, permute, share):
+        def interleave(raw, cut, last):
             width = raw.shape[2]
-            grouped = work.tile([P, width * PACK], BF16, name=f"grouped{width}", align_bytes=64)
-            if permute:
-                to = grouped[:].rearrange("p (t m i j) -> p m j t i", t=4, i=2, j=PACK)
-                fro = raw.rearrange("p j (m i t) -> p m j t i", t=4, i=2)
-            else:
-                to = grouped[:].rearrange("p (c i j) -> p c j i", i=4, j=PACK)
-                fro = raw.rearrange("p j (c i) -> p c j i", i=4)
-            blocks = to.shape[1]
-            cut = blocks * share // 256 * 2
+            grouped = work.tile([P, width * PACK], BF16, name=f"grouped{width}", tag="last" if last else f"grouped{width}", align_bytes=64, bufs=1 if last else {512: 4, 256: 4, 128: 2}[width])
+            to = grouped[:].rearrange("p (c i j) -> p c j i", i=RUN, j=PACK)
+            fro = raw.rearrange("p j (c i) -> p c j i", i=RUN)
             if cut > 0:
-                nc.vector.tensor_copy(to[:, :cut], fro[:, :cut])
-            if cut < blocks:
-                nc.scalar.copy(to[:, cut:], fro[:, cut:])
+                nc.vector.tensor_copy(to[:, :cut // RUN], fro[:, :cut // RUN])
+            if cut < width:
+                nc.scalar.copy(to[:, cut // RUN:], fro[:, cut // RUN:])
             return grouped
 
-        def quantize(grouped, codes, scales):
-            nc.vector.quantize_mx(out=codes.bitcast(FP8X4), scales=scales, in_=grouped[:])
+        def quantize(values, codes, scales):
+            nc.vector.quantize_mx(out=codes.bitcast(FP8X4), scales=scales, in_=values)
 
-        def x_scales(s):
-            return bytes_slot[s // 4], 4 * (s % 4)
-
-        def banks(base):
-            return [psum.tile([P, 512], F32, tag=f"bank{base + t}", name=f"acc{base + t}") for t in range(4)]
+        def bank(b, name):
+            return psum.tile([P, 512], F32, tag=f"bank{b}", name=name)
 
         def gather_words(s, e):
             nc.vector.tensor_copy(words_slot[s][:, e * C:(e + 1) * C], words_all[s][:].indirect(offs_sb[:, e * 16:(e + 1) * 16]))
@@ -102,173 +95,172 @@ def tile_moe_two_glu_sigmoid_kernel(tc, xT, w1, w3, w2, gate, offs, dst, out):
         def gather_bytes(g, e):
             nc.vector.tensor_copy(bytes_slot[g][:, e * C:(e + 1) * C], bytes_all[g][:].indirect(offs_sb[:, e * 16:(e + 1) * 16]))
 
-        def multiply(acc, codes, scales, s, e):
-            plane, k = x_scales(s)
-            cols = slice(e * C, (e + 1) * C)
-            for t in range(4):
-                m = slice(t * P, (t + 1) * P)
-                nc.tensor.matmul_mx(
-                    out=acc[t][:, :C],
-                    lhsT=codes[:, m].bitcast(FP8X4),
-                    lhsT_scale=scales[:, m],
-                    rhs=words_slot[s][:, cols].bitcast(FP8X4),
-                    rhs_scale=plane[k:P, cols],
-                    start=(s == 0),
-                    stop=(s == PASSES - 1),
-                )
+        def column_groups(kind, e, u, cols):
+            groups = GROUPS[u] if (kind, e) == ("w3", E - 1) else [WHOLE]
+            return [(v, lo, hi) for v, (lo, hi) in enumerate(groups) if cols[0] < hi <= cols[1]]
 
-        groups = [[("x", 0, 0)], [("w1", 0, 0)]]
-        for s in range(1, PASSES):
-            groups += [[("x", 0, s)], [("w1", 0, s)]]
-        for kind, e in (("w3", 0), ("w1", 1), ("w3", 1)):
-            groups += [[(kind, e, s)] for s in range(PASSES)]
-            if kind == "w3":
-                groups.append([("w2", e, 0)])
+        def by_word(flat):
+            return flat.rearrange("s (p w i) -> s w p i", w=2, i=2)
 
-        weights = {"w1": w1, "w3": w3, "w2": w2}
-        made = {}
-        acc = {}
-        sig = {}
-
-        def after(kind, e, s):
-            if kind == "x":
-                gather_words(s, 0)
-                if s == 3:
-                    gather_bytes(0, 0)
-                if s == PASSES - 1:
-                    gather_bytes(1, 0)
-                return
-            if kind == "w2":
-                return
-            if kind == "w1" and e == 0:
-                if s < PASSES - 1:
-                    return
-                acc["w1"] = banks(0)
-                for r in range(PASSES):
-                    multiply(acc["w1"], *made["w1", 0, r], r, 0)
-            else:
-                if s == 0:
-                    acc[kind] = banks(0 if kind == "w1" else 4)
-                multiply(acc[kind], *made[kind, e, s], s, e)
-            if kind == "w3" and e == 0:
-                gather_words(s, 1)
-                if s < 2:
-                    gather_bytes(s, 1)
-            if s == PASSES - 1:
-                if kind == "w1":
-                    sig[e] = keep.tile([P, 4, C], F32, name=f"sig{e}")
-                    for t in range(4):
-                        nc.scalar.activation(sig[e][:, t, :], acc["w1"][t][:, :C], SIGMOID)
-                else:
-                    hidden(e)
-
-        def parts(e):
-            return 1 if e == 0 else 2
-
-        def hidden(e):
-            n_parts = parts(e)
-            width = C // n_parts
-            made["h", e] = []
-            tiles = []
-            for u in range(n_parts):
-                cols = slice(u * width, (u + 1) * width)
-                hb = keep.tile([P, 4, width], BF16, name=f"hb{e}{u}")
-                for t in range(4):
-                    nc.vector.tensor_tensor(hb[:, t, :], acc["w3"][t][:, cols], sig[e][:, t, cols], MULT)
-                hi = keep.tile([P, width * 4], BF16, name=f"hi{e}{u}", align_bytes=64)
-                tiles.append((hb, hi))
-                if e == 1 and u == 0:
-                    g, c, sc = waiting.pop(0)[:3]
-                    quantize(g, c, sc)
-                    nc.scalar.copy(hi[:].rearrange("p (c i t) -> p c t i", i=4, t=4), hb[:].rearrange("p t (c i) -> p c t i", i=4))
-            for u in range(n_parts):
-                hb, hi = tiles[u]
-                if not (e == 1 and u == 0):
-                    nc.vector.tensor_copy(hi[:].rearrange("p (c i t) -> p c t i", i=4, t=4), hb[:].rearrange("p t (c i) -> p c t i", i=4))
-                codes = keep.tile([P, width], U32, name=f"h_codes{e}{u}", align_bytes=64)
-                scales = keep.tile([P, width], U8, name=f"h_scales{e}{u}", align_bytes=64)
-                quantize(hi, codes[:], scales[:])
-                made["h", e].append((codes, scales))
-
-        def second(e):
-            n_parts = parts(e)
-            width = C // n_parts
-            codes, scales = made["w2", e, 0]
-            for u in range(n_parts):
-                h_codes, h_scales = made["h", e][u]
-                b = (4 if e == 0 else 0) + u
-                y = psum.tile([P, 512], F32, tag=f"bank{b}", name=f"y{e}{u}")
-                for q in range(N // P):
-                    n = slice(q * P, (q + 1) * P)
+        def first_layer(kind, e, s, cols):
+            codes, scales = made[kind, e, s]
+            for u in range(2):
+                for v, lo, hi in column_groups(kind, e, u, cols):
+                    if s == 0:
+                        acc[kind, u, v] = bank(u if kind == "w1" else 2 + 3 * u + v, f"{kind}{e}{u}{v}")
+                    slots = slice(e * C + u * P, e * C + (u + 1) * P)
                     nc.tensor.matmul_mx(
-                        out=y[:, q * width:(q + 1) * width],
-                        lhsT=codes[:, n].bitcast(FP8X4),
-                        lhsT_scale=scales[:, n],
-                        rhs=h_codes[:].bitcast(FP8X4),
-                        rhs_scale=h_scales[:],
-                        start=True,
-                        stop=True,
+                        out=acc[kind, u, v][:, :hi - lo],
+                        lhsT=words_slot[s][:, slots].bitcast(FP8X4),
+                        lhsT_scale=bytes_slot[s // 4][4 * (s % 4):P, slots],
+                        rhs=codes[:, lo:hi].bitcast(FP8X4),
+                        rhs_scale=scales[:, lo:hi],
+                        start=(s == 0),
+                        stop=(s == PASSES - 1),
                     )
-                ysb = keep.tile([P, 2, width], F32, name=f"ysb{e}{u}")
-                nc.scalar.copy(ysb[:], y[:, :2 * width].rearrange("p (q c) -> p q c", q=2))
-                first = e * 16 + u * (width // 16)
-                for q in range(N // P):
-                    nc.vector.tensor_tensor(placed[q][:].indirect(dst_sb[:, first:first + width // 16]), ysb[:, q, :], gate_sb[e][:, q, u * width:(u + 1) * width], MULT)
-                    if e == E - 1 and u == n_parts - 1:
-                        nc.sync.dma_start(out[q * P:(q + 1) * P, :], placed[q][:])
+
+        def sigmoids():
+            for u in range(2):
+                sig[u] = keep.tile([P, 2, P, 2], F32, name=f"sig{u}")
+                nc.scalar.activation(sig[u][:], by_word(acc["w1", u, 0][:]), SIGMOID)
+
+        def product(e, u, cols):
+            hidden[u] = work.tile([P, 2, P, 2], BF16, name=f"hidden{u}", tag="last" if (e, u) == (E - 1, 0) else f"hidden{u}", align_bytes=64)
+            for v, lo, hi in column_groups("w3", e, u, cols):
+                part = slice(lo // PACK, hi // PACK)
+                nc.vector.tensor_tensor(hidden[u][:, :, part], by_word(acc["w3", u, v][:, :hi - lo]), sig[u][:, :, part], MULT)
+
+        def turn(e, u):
+            words = hidden[u][:].rearrange("s w p i -> s (w p i)").bitcast(F32)
+            turned = bank(2 + 3 * u, f"turned{e}{u}")
+            for w in range(2):
+                nc.tensor.transpose(turned[:, w * P:(w + 1) * P], words[:, w * P:(w + 1) * P], identity[:])
+            woven[u] = keep.tile([P, P * PACK], BF16, name=f"woven{u}", align_bytes=64)
+            nc.scalar.copy(woven[u][:].bitcast(F32).rearrange("p (c w) -> p c w", w=2), turned[:, :2 * P].rearrange("p (w c) -> p c w", w=2))
+
+        def quantize_hidden(e, u):
+            codes = keep.tile([P, P], U32, name=f"h_codes{u}", align_bytes=64)
+            scales = keep.tile([P, P], U8, name=f"h_scales{u}", align_bytes=64)
+            quantize(woven[u][:], codes[:], scales[:])
+            made["h", e, u] = (codes, scales)
+
+        def second_layer(e, u):
+            codes, scales = made["w2", e, 0]
+            h_codes, h_scales = made["h", e, u]
+            results[u] = []
+            for q in range(N // P):
+                n = slice(q * P, (q + 1) * P)
+                y = bank(3 + 3 * u + q, f"y{e}{u}{q}")
+                nc.tensor.matmul_mx(
+                    out=y[:, :P],
+                    lhsT=codes[:, n].bitcast(FP8X4),
+                    lhsT_scale=scales[:, n],
+                    rhs=h_codes[:].bitcast(FP8X4),
+                    rhs_scale=h_scales[:],
+                    start=True,
+                    stop=True,
+                )
+                ysb = keep.tile([P, P], F32, name=f"ysb{u}{q}")
+                nc.scalar.copy(ysb[:], y[:, :P])
+                results[u].append(ysb)
+
+        def scatter(e, u, q):
+            first = e * 16 + u * 8
+            nc.vector.tensor_tensor(placed[q][:].indirect(dst_sb[:, first:first + 8]), results[u][q][:], gate_sb[e][:, u * P:(u + 1) * P], MULT)
+
+        def fetch(kind, e, first, count=1, cols=WHOLE):
+            raw = load(kind, e, first, count, cols)
+            for a in range(count):
+                raws[kind, e, first + a, cols] = raw[:, a]
+
+        def weave(kind, e, s, cols=WHOLE, cut=None):
+            if (kind, e, s, cols) not in raws:
+                fetch(kind, e, s, PAIRED.get((kind, e, s), 1), cols)
+            grouped = interleave(raws[kind, e, s, cols], VECTOR_COLUMNS[kind, e][s] if cut is None else cut, (s, cols) == LAST_PIECES[-1][:2])
+            if kind == "x":
+                return grouped, words_all[s][:], bytes_all[s // 4][4 * (s % 4):P, :]
+            if (kind, e, s) not in made:
+                width = N if kind == "w2" else H
+                codes_t = work.tile([P, width], U32, name=f"codes{width}", align_bytes=64, bufs=8 if width == H else 2)
+                scales_t = work.tile([P, width], U8, name=f"scales{width}", align_bytes=64, bufs=8 if width == H else 2)
+                made[kind, e, s] = (codes_t, scales_t)
+            return (grouped,) + tuple(t[:, cols[0]:cols[1]] for t in made[kind, e, s])
+
+        def pack(job):
+            quantize(job[0][:], job[1], job[2])
 
         def load_gate(e):
-            nc.sync.dma_start(gate_sb[e][:], gate[:, e * C:(e + 1) * C].rearrange("(q p) s -> p q s", p=P))
+            nc.sync.dma_start(gate_sb[e][:], gate[:P, e * C:(e + 1) * C])
 
-        raws = {}
-        waiting = []
-
-        def load_group(i, group):
-            kind, e, s = group[0]
-            source = xT if kind == "x" else weights[kind][e]
-            rows = source[s * K_PASS:(s + len(group)) * K_PASS, :]
-            if group == [("w3", 1, PASSES - 1)]:
-                raws[group[0]] = load_halves(rows)
-            else:
-                for key, raw in zip(group, load(rows)):
-                    raws[key] = raw
-            if i == 0:
+        for s in range(PASSES):
+            job = weave("x", 0, s)
+            if s == 0:
                 nc.sync.dma_start(offs_sb[:], offs)
-            if kind == "w2":
-                if e == 0:
-                    nc.sync.dma_start(dst_sb[:], dst)
-                load_gate(e)
-
-        def process(kind, e, s):
-            raw = raws[kind, e, s]
-            if (kind, e, s) == ("w3", 1, PASSES - 1):
-                grouped = interleave_halves(raw)
             else:
-                grouped = interleave(raw, kind in ("w1", "w3"), VECTOR_SHARE[kind, e])
-            if kind == "x":
-                k = 4 * (s % 4)
-                codes, scales = words_all[s][:], bytes_all[s // 4][k:P, :]
-            else:
-                width = N if kind == "w2" else H
-                codes_t = keep.tile([P, width], U32, name=f"{kind}c{e}{s}", align_bytes=64)
-                scales_t = keep.tile([P, width], U8, name=f"{kind}s{e}{s}", align_bytes=64)
-                made[kind, e, s] = (codes_t, scales_t)
-                codes, scales = codes_t[:], scales_t[:]
-            waiting.append((grouped, codes, scales, kind, e, s))
-            if len(waiting) > 1:
-                g, c, sc, kd, ee, ss = waiting.pop(0)
-                if (kd, ee, ss) == ("w3", 1, PASSES - 1):
-                    for t in range(4):
-                        m = slice(t * P, (t + 1) * P)
-                        nc.vector.quantize_mx(out=c[:, m].bitcast(FP8X4), scales=sc[:, m], in_=g[:, t * 512:(t + 1) * 512])
-                else:
-                    quantize(g, c, sc)
-                after(kd, ee, ss)
-                if kd == "w2" and ee == 0:
-                    second(0)
-
-        for i, group in enumerate(groups):
-            load_group(i, group)
-            for key in group:
-                process(*key)
-        second(1)
+                gather_words(s - 1, 1)
+            if s == 4:
+                gather_bytes(0, 1)
+            pack(job)
+            job = weave("w1", 0, s)
+            gather_words(s, 0)
+            if s >= 3:
+                gather_bytes(s - 3, 0)
+            pack(job)
+            if s >= 3:
+                for r in (range(4) if s == 3 else [4]):
+                    first_layer("w1", 0, r, WHOLE)
+        for s in range(PASSES):
+            job = weave("w3", 0, s)
+            if s == 0:
+                gather_words(4, 1)
+                gather_bytes(1, 1)
+            if s == 1:
+                sigmoids()
+            pack(job)
+            first_layer("w3", 0, s, WHOLE)
+        job = weave("w2", 0, 0, cols=(0, N))
+        nc.sync.dma_start(dst_sb[:], dst)
+        load_gate(0)
+        pack(job)
+        for u in range(2):
+            product(0, u, WHOLE)
+            turn(0, u)
+        for s in range(PASSES):
+            job = weave("w1", 1, s)
+            if s == 0:
+                for u in range(2):
+                    quantize_hidden(0, u)
+                    second_layer(0, u)
+            if s in (1, 2):
+                for q in range(2):
+                    scatter(0, s - 1, q)
+            pack(job)
+            first_layer("w1", 1, s, WHOLE)
+        for s in range(LAST_PIECES[0][0]):
+            job = weave("w3", 1, s)
+            if s == 0:
+                sigmoids()
+            pack(job)
+            first_layer("w3", 1, s, WHOLE)
+        for s, cols, cut in LAST_PIECES[:-2]:
+            pack(weave("w3", 1, s, cols=cols, cut=cut))
+            first_layer("w3", 1, s, cols)
+        jobs = [weave("w3", 1, s, cols=cols, cut=cut) for s, cols, cut in LAST_PIECES[-2:]]
+        for job, (s, cols, cut) in zip(jobs, LAST_PIECES[-2:]):
+            pack(job)
+            first_layer("w3", 1, s, cols)
+        job = weave("w2", 1, 0, cols=(0, N))
+        load_gate(1)
+        product(1, 0, WHOLE)
+        turn(1, 0)
+        product(1, 1, WHOLE)
+        turn(1, 1)
+        pack(job)
+        for u in range(2):
+            quantize_hidden(1, u)
+            second_layer(1, u)
+        for u in range(2):
+            for q in range(2):
+                scatter(1, u, q)
+                if u == 1:
+                    nc.sync.dma_start(out[q * P:(q + 1) * P, :], placed[q][:])

@@ -19,11 +19,11 @@ FP8X4 = mybir.dt.float8_e4m3fn_x4
 SIGMOID = mybir.ActivationFunctionType.Sigmoid
 MULT = mybir.AluOpType.mult
 
-PAIRED = {}
+PAIRED = {("x", 0, 1): 2, ("x", 0, 3): 2, ("w1", 0, 0): 2, ("w1", 0, 2): 2, ("w3", 0, 0): 2}
 RUN = 4
 WHOLE = (0, H)
 GROUPS = [[(0, 256), (256, 384), (384, 512)], [WHOLE]]
-VECTOR_COLUMNS = {("x", 0): (128,) * 5, ("w1", 0): (128,) * 5, ("w3", 0): (256,) * 5, ("w2", 0): (80,) * 5, ("w1", 1): (128,) * 5, ("w3", 1): (336,) * 5, ("w2", 1): (0,) * 5}
+VECTOR_COLUMNS = {("x", 0): (64,) * 5, ("w1", 0): (192,) * 5, ("w3", 0): (256,) * 5, ("w2", 0): (64,) * 5, ("w1", 1): (128,) * 5, ("w3", 1): (336,) * 5, ("w2", 1): (0,) * 5}
 LAST_PIECES = [(3, (0, 256), 96), (3, (256, 512), 96), (4, (0, 256), 96), (4, (256, 384), 0), (4, (384, 512), 64)]
 
 
@@ -38,11 +38,6 @@ def tile_moe_two_glu_sigmoid_kernel(tc, xT, w1, w3, w2, gate, offs, dst, out):
 
         offs_sb = lists.tile([P, E * C // 16], U16, name="offs_sb")
         dst_sb = lists.tile([P, E * C // 16], U16, name="dst_sb")
-
-        warm_in = keep.tile([P, 1], F32, name="warm_in")
-        warm_out = keep.tile([P, 1], F32, name="warm_out")
-        nc.vector.memset(warm_in[:], 0.0)
-        nc.scalar.activation(warm_out[:], warm_in[:], SIGMOID)
 
         bytes_all = [keep.tile([P, T], U8, name=f"bytes_all{g}", align_bytes=64) for g in range(2)]
         bytes_slot = [keep.tile([P, E * C], U8, name=f"bytes_slot{g}", align_bytes=64) for g in range(2)]
@@ -68,7 +63,7 @@ def tile_moe_two_glu_sigmoid_kernel(tc, xT, w1, w3, w2, gate, offs, dst, out):
             source = xT if kind == "x" else weights[kind][e]
             rows = source[first * K_PASS:(first + count) * K_PASS, cols[0]:cols[1]]
             width = cols[1] - cols[0]
-            raw = stage.tile([P, count, PACK, width], F32, name=f"raw{count}_{width}", bufs={(1, 512): 8, (1, 256): 5, (1, 128): 2}[count, width])
+            raw = stage.tile([P, count, PACK, width], F32, name=f"raw{count}_{width}", bufs={(1, 512): 7, (2, 512): 4, (1, 256): 5, (1, 128): 2}[count, width])
             nc.sync.dma_start(raw[:], rows.rearrange("(a p j) w -> p a j w", p=P, j=PACK))
             return raw
 
@@ -196,28 +191,18 @@ def tile_moe_two_glu_sigmoid_kernel(tc, xT, w1, w3, w2, gate, offs, dst, out):
             job = weave("x", 0, s)
             if s == 0:
                 nc.sync.dma_start(offs_sb[:], offs)
-            else:
-                gather_words(s - 1, 1)
-            if s == 4:
-                gather_bytes(0, 1)
             pack(job)
-            job = weave("w1", 0, s)
-            gather_words(s, 0)
-            if s >= 3:
-                gather_bytes(s - 3, 0)
-            pack(job)
-            if s >= 3:
-                for r in (range(4) if s == 3 else [4]):
-                    first_layer("w1", 0, r, WHOLE)
-        for s in range(PASSES):
-            job = weave("w3", 0, s)
-            if s == 0:
-                gather_words(4, 1)
-                gather_bytes(1, 1)
-            if s == 1:
-                sigmoids()
-            pack(job)
-            first_layer("w3", 0, s, WHOLE)
+            for e in range(E):
+                gather_words(s, e)
+                if s >= 3:
+                    gather_bytes(s - 3, e)
+        for kind in ("w1", "w3"):
+            for s in range(PASSES):
+                job = weave(kind, 0, s)
+                if (kind, s) == ("w3", 0):
+                    sigmoids()
+                pack(job)
+                first_layer(kind, 0, s, WHOLE)
         job = weave("w2", 0, 0, cols=(0, N))
         nc.sync.dma_start(dst_sb[:], dst)
         load_gate(0)

@@ -8,6 +8,10 @@ P = 128
 PACK = 4
 K_PASS = P * PACK
 PASSES = K // K_PASS
+PLANES = 4
+LIST = 16
+SLOT_TILES = C // P
+ROW_TILES = N // P
 FLOPS = 2 * E * C * (2 * K * H + H * N)
 
 F32 = mybir.dt.float32
@@ -19,12 +23,13 @@ FP8X4 = mybir.dt.float8_e4m3fn_x4
 SIGMOID = mybir.ActivationFunctionType.Sigmoid
 MULT = mybir.AluOpType.mult
 
-PAIRED = {("x", 0, 1): 2, ("x", 0, 3): 2, ("w1", 0, 0): 2, ("w1", 0, 2): 2, ("w3", 0, 0): 2}
-RUN = 4
-WHOLE = (0, H)
-GROUPS = [[(0, 256), (256, 384), (384, 512)], [WHOLE]]
-VECTOR_COLUMNS = {("x", 0): (64,) * 5, ("w1", 0): (192,) * 5, ("w3", 0): (256,) * 5, ("w2", 0): (64,) * 5, ("w1", 1): (128,) * 5, ("w3", 1): (336,) * 5, ("w2", 1): (0,) * 5}
-LAST_PIECES = [(3, (0, 256), 96), (3, (256, 512), 96), (4, (0, 256), 96), (4, (256, 384), 0), (4, (384, 512), 64)]
+RUN = 2
+ALL = slice(0, H)
+LEFT, RIGHT = slice(0, H // 2), slice(H // 2, H)
+
+VECTOR_COLUMNS = {("x", 0): 64, ("w1", 0): 192, ("w3", 0): 256, ("w2", 0): 64, ("w1", 1): 128, ("w3", 1): 336, ("w2", 1): 0}
+
+A_BANK, B_BANK, TURN_BANK = 0, 2, 6
 
 
 def tile_moe_two_glu_sigmoid_kernel(tc, xT, w1, w3, w2, gate, offs, dst, out):
@@ -32,220 +37,193 @@ def tile_moe_two_glu_sigmoid_kernel(tc, xT, w1, w3, w2, gate, offs, dst, out):
     with ExitStack() as ctx:
         lists = ctx.enter_context(tc.tile_pool(name="lists", bufs=1))
         keep = ctx.enter_context(tc.tile_pool(name="keep", bufs=1))
-        stage = ctx.enter_context(tc.tile_pool(name="stage", bufs=1))
-        work = ctx.enter_context(tc.tile_pool(name="work", bufs=1))
+        stage = ctx.enter_context(tc.tile_pool(name="stage", bufs=8))
+        work = ctx.enter_context(tc.tile_pool(name="work", bufs=4))
         psum = ctx.enter_context(tc.psum_pool(name="psum", bufs=1))
 
-        offs_sb = lists.tile([P, E * C // 16], U16, name="offs_sb")
-        dst_sb = lists.tile([P, E * C // 16], U16, name="dst_sb")
+        offs_sb = lists.tile([P, E * C // LIST], U16, name="offs_sb")
+        dst_sb = lists.tile([P, E * C // LIST], U16, name="dst_sb")
 
-        bytes_all = [keep.tile([P, T], U8, name=f"bytes_all{g}", align_bytes=64) for g in range(2)]
-        bytes_slot = [keep.tile([P, E * C], U8, name=f"bytes_slot{g}", align_bytes=64) for g in range(2)]
-        for b in bytes_all:
-            nc.gpsimd.memset(b[:], 0)
+        scale_tiles = (PASSES + PLANES - 1) // PLANES
+        token_scales = [keep.tile([P, T], U8, name=f"token_scales{g}", align_bytes=64) for g in range(scale_tiles)]
+        slot_scales = [keep.tile([P, E * C], U8, name=f"slot_scales{g}", align_bytes=64) for g in range(scale_tiles)]
+        for plane in token_scales:
+            nc.gpsimd.memset(plane[:], 0)
         identity = keep.tile([P, P], F32, name="identity")
         make_identity(nc, identity[:])
-        words_all = [keep.tile([P, T], U32, name=f"words_all{s}", align_bytes=64) for s in range(PASSES)]
-        words_slot = [keep.tile([P, E * C], U32, name=f"words_slot{s}", align_bytes=64) for s in range(PASSES)]
-        gate_sb = [keep.tile([P, C], F32, name=f"gate_sb{e}") for e in range(E)]
-        placed = [keep.tile([P, T], F32, name=f"placed{q}") for q in range(N // P)]
+        token_words = [keep.tile([P, T], U32, name=f"token_words{s}", align_bytes=64) for s in range(PASSES)]
+        slot_words = [keep.tile([P, E * C], U32, name=f"slot_words{s}", align_bytes=64) for s in range(PASSES)]
+        placed = [keep.tile([P, T], F32, name=f"placed{q}") for q in range(ROW_TILES)]
 
-        weights = {"w1": w1, "w3": w3, "w2": w2}
-        made = {}
-        acc = {}
-        sig = {}
-        hidden = {}
-        woven = {}
-        results = {}
-        raws = {}
-
-        def load(kind, e, first, count, cols):
-            source = xT if kind == "x" else weights[kind][e]
-            rows = source[first * K_PASS:(first + count) * K_PASS, cols[0]:cols[1]]
-            width = cols[1] - cols[0]
-            raw = stage.tile([P, count, PACK, width], F32, name=f"raw{count}_{width}", bufs={(1, 512): 7, (2, 512): 4, (1, 256): 5, (1, 128): 2}[count, width])
-            nc.sync.dma_start(raw[:], rows.rearrange("(a p j) w -> p a j w", p=P, j=PACK))
+        def load_pass(matrix, s):
+            width = matrix.shape[1]
+            raw = stage.tile([P, PACK, width], F32, name=f"raw{width}", bufs=8 if width == H else E)
+            nc.sync.dma_start(raw[:], matrix[s * K_PASS:(s + 1) * K_PASS, :].rearrange("(p j) w -> p j w", j=PACK))
             return raw
 
-        def interleave(raw, cut, last):
-            width = raw.shape[2]
-            grouped = work.tile([P, width * PACK], BF16, name=f"grouped{width}", tag="last" if last else f"grouped{width}", align_bytes=64, bufs=1 if last else {512: 4, 256: 4, 128: 2}[width])
+        def weave(copy, grouped, raw, columns, rows):
+            runs = slice(columns.start // RUN, columns.stop // RUN)
             to = grouped[:].rearrange("p (c i j) -> p c j i", i=RUN, j=PACK)
-            fro = raw.rearrange("p j (c i) -> p c j i", i=RUN)
+            copy(to[:, runs, rows], raw[:].rearrange("p j (c i) -> p c j i", i=RUN)[:, runs])
+
+        def interleave(raw, cut):
+            width = raw.shape[2]
+            grouped = work.tile([P, width * PACK], BF16, name=f"grouped{width}", align_bytes=64)
             if cut > 0:
-                nc.vector.tensor_copy(to[:, :cut // RUN], fro[:, :cut // RUN])
-            if cut < width:
-                nc.scalar.copy(to[:, cut // RUN:], fro[:, cut // RUN:])
+                weave(nc.vector.tensor_copy, grouped, raw, slice(0, cut), slice(0, PACK))
+            weave(nc.scalar.copy, grouped, raw, slice(cut, width), slice(0, PACK))
             return grouped
 
         def quantize(values, codes, scales):
             nc.vector.quantize_mx(out=codes.bitcast(FP8X4), scales=scales, in_=values)
 
+        def packed(width, name):
+            codes = work.tile([P, width], U32, name=f"{name}_codes", align_bytes=64)
+            scales = work.tile([P, width], U8, name=f"{name}_scales", align_bytes=64)
+            return codes, scales
+
         def bank(b, name):
             return psum.tile([P, 512], F32, tag=f"bank{b}", name=name)
 
-        def gather_words(s, e):
-            nc.vector.tensor_copy(words_slot[s][:, e * C:(e + 1) * C], words_all[s][:].indirect(offs_sb[:, e * 16:(e + 1) * 16]))
+        def gather(slots, tokens, e):
+            nc.vector.tensor_copy(slots[:, e * C:(e + 1) * C], tokens[:].indirect(offs_sb[:, e * C // LIST:(e + 1) * C // LIST]))
 
-        def gather_bytes(g, e):
-            nc.vector.tensor_copy(bytes_slot[g][:, e * C:(e + 1) * C], bytes_all[g][:].indirect(offs_sb[:, e * 16:(e + 1) * 16]))
+        def multiply(acc, weights, e, u, s, columns):
+            codes, scales = weights
+            slots = slice(e * C + u * P, e * C + (u + 1) * P)
+            nc.tensor.matmul_mx(
+                out=acc[:, :columns.stop - columns.start],
+                lhsT=slot_words[s][:, slots].bitcast(FP8X4),
+                lhsT_scale=slot_scales[s // PLANES][4 * (s % PLANES):P, slots],
+                rhs=codes[:, columns].bitcast(FP8X4),
+                rhs_scale=scales[:, columns],
+                start=(s == 0),
+                stop=(s == PASSES - 1),
+            )
 
-        def column_groups(kind, e, u, cols):
-            groups = GROUPS[u] if (kind, e) == ("w3", E - 1) else [WHOLE]
-            return [(v, lo, hi) for v, (lo, hi) in enumerate(groups) if cols[0] < hi <= cols[1]]
+        def first_layer_pass(name, matrix, e, s, groups):
+            grouped = interleave(load_pass(matrix[e], s), VECTOR_COLUMNS[name, e])
+            weights = packed(H, "weight")
+            quantize(grouped[:], weights[0][:], weights[1][:])
+            for u, columns, acc in groups:
+                multiply(acc, weights, e, u, s, columns)
 
-        def by_word(flat):
-            return flat.rearrange("s (p w i) -> s w p i", w=2, i=2)
+        def by_pair(columns):
+            return columns.rearrange("s (p w r) -> s w p r", w=2, r=2)
 
-        def first_layer(kind, e, s, cols):
-            codes, scales = made[kind, e, s]
-            for u in range(2):
-                for v, lo, hi in column_groups(kind, e, u, cols):
-                    if s == 0:
-                        acc[kind, u, v] = bank(u if kind == "w1" else 2 + 3 * u + v, f"{kind}{e}{u}{v}")
-                    slots = slice(e * C + u * P, e * C + (u + 1) * P)
-                    nc.tensor.matmul_mx(
-                        out=acc[kind, u, v][:, :hi - lo],
-                        lhsT=words_slot[s][:, slots].bitcast(FP8X4),
-                        lhsT_scale=bytes_slot[s // 4][4 * (s % 4):P, slots],
-                        rhs=codes[:, lo:hi].bitcast(FP8X4),
-                        rhs_scale=scales[:, lo:hi],
-                        start=(s == 0),
-                        stop=(s == PASSES - 1),
-                    )
+        def sigmoids(groups):
+            sig = [keep.tile([P, 2, P, 2], F32, name=f"sig{u}") for u in range(SLOT_TILES)]
+            for u, columns, acc in groups:
+                nc.scalar.activation(sig[u][:], by_pair(acc[:, columns]), SIGMOID)
+            return sig
 
-        def sigmoids():
-            for u in range(2):
-                sig[u] = keep.tile([P, 2, P, 2], F32, name=f"sig{u}")
-                nc.scalar.activation(sig[u][:], by_word(acc["w1", u, 0][:]), SIGMOID)
-
-        def product(e, u, cols):
-            hidden[u] = work.tile([P, 2, P, 2], BF16, name=f"hidden{u}", tag="last" if (e, u) == (E - 1, 0) else f"hidden{u}", align_bytes=64)
-            for v, lo, hi in column_groups("w3", e, u, cols):
-                part = slice(lo // PACK, hi // PACK)
-                nc.vector.tensor_tensor(hidden[u][:, :, part], by_word(acc["w3", u, v][:, :hi - lo]), sig[u][:, :, part], MULT)
-
-        def turn(e, u):
-            words = hidden[u][:].rearrange("s w p i -> s (w p i)").bitcast(F32)
-            turned = bank(2 + 3 * u, f"turned{e}{u}")
+        def hidden_values(u, groups, sig):
+            hidden = keep.tile([P, 2, P, 2], BF16, name=f"hidden{u}")
+            for tile, columns, acc in groups:
+                if tile == u:
+                    words = slice(columns.start // PACK, columns.stop // PACK)
+                    nc.vector.tensor_tensor(hidden[:, :, words], by_pair(acc[:, :columns.stop - columns.start]), sig[u][:, :, words], MULT)
+            pairs = hidden[:].rearrange("s w p r -> s (w p r)").bitcast(F32)
+            turned = bank(TURN_BANK + u, f"turned{u}")
             for w in range(2):
-                nc.tensor.transpose(turned[:, w * P:(w + 1) * P], words[:, w * P:(w + 1) * P], identity[:])
-            woven[u] = keep.tile([P, P * PACK], BF16, name=f"woven{u}", align_bytes=64)
-            nc.scalar.copy(woven[u][:].bitcast(F32).rearrange("p (c w) -> p c w", w=2), turned[:, :2 * P].rearrange("p (w c) -> p c w", w=2))
+                nc.tensor.transpose(turned[:, w * P:(w + 1) * P], pairs[:, w * P:(w + 1) * P], identity[:])
+            woven = keep.tile([P, P * PACK], BF16, name=f"woven{u}", align_bytes=64)
+            nc.scalar.copy(woven[:].bitcast(F32).rearrange("p (c w) -> p c w", w=2), turned[:, :2 * P].rearrange("p (w c) -> p c w", w=2))
+            return woven
 
-        def quantize_hidden(e, u):
-            codes = keep.tile([P, P], U32, name=f"h_codes{u}", align_bytes=64)
-            scales = keep.tile([P, P], U8, name=f"h_scales{u}", align_bytes=64)
-            quantize(woven[u][:], codes[:], scales[:])
-            made["h", e, u] = (codes, scales)
-
-        def second_layer(e, u):
-            codes, scales = made["w2", e, 0]
-            h_codes, h_scales = made["h", e, u]
-            results[u] = []
-            for q in range(N // P):
-                n = slice(q * P, (q + 1) * P)
-                y = bank(3 + 3 * u + q, f"y{e}{u}{q}")
+        def second_layer(u, weights, woven):
+            codes, scales = weights
+            h_codes, h_scales = packed(P, "hidden")
+            quantize(woven[:], h_codes[:], h_scales[:])
+            results = []
+            for q in range(ROW_TILES):
+                rows = slice(q * P, (q + 1) * P)
+                y = bank(B_BANK + ROW_TILES * u + q, f"y{u}{q}")
                 nc.tensor.matmul_mx(
                     out=y[:, :P],
-                    lhsT=codes[:, n].bitcast(FP8X4),
-                    lhsT_scale=scales[:, n],
+                    lhsT=codes[:, rows].bitcast(FP8X4),
+                    lhsT_scale=scales[:, rows],
                     rhs=h_codes[:].bitcast(FP8X4),
                     rhs_scale=h_scales[:],
                     start=True,
                     stop=True,
                 )
-                ysb = keep.tile([P, P], F32, name=f"ysb{u}{q}")
-                nc.scalar.copy(ysb[:], y[:, :P])
-                results[u].append(ysb)
+                result = keep.tile([P, P], F32, name=f"result{u}{q}")
+                nc.scalar.copy(result[:], y[:, :P])
+                results.append(result)
+            return results
 
-        def scatter(e, u, q):
-            first = e * 16 + u * 8
-            nc.vector.tensor_tensor(placed[q][:].indirect(dst_sb[:, first:first + 8]), results[u][q][:], gate_sb[e][:, u * P:(u + 1) * P], MULT)
-
-        def fetch(kind, e, first, count=1, cols=WHOLE):
-            raw = load(kind, e, first, count, cols)
-            for a in range(count):
-                raws[kind, e, first + a, cols] = raw[:, a]
-
-        def weave(kind, e, s, cols=WHOLE, cut=None):
-            if (kind, e, s, cols) not in raws:
-                fetch(kind, e, s, PAIRED.get((kind, e, s), 1), cols)
-            grouped = interleave(raws[kind, e, s, cols], VECTOR_COLUMNS[kind, e][s] if cut is None else cut, (s, cols) == LAST_PIECES[-1][:2])
-            if kind == "x":
-                return grouped, words_all[s][:], bytes_all[s // 4][4 * (s % 4):P, :]
-            if (kind, e, s) not in made:
-                width = N if kind == "w2" else H
-                codes_t = work.tile([P, width], U32, name=f"codes{width}", align_bytes=64, bufs=8 if width == H else 2)
-                scales_t = work.tile([P, width], U8, name=f"scales{width}", align_bytes=64, bufs=8 if width == H else 2)
-                made[kind, e, s] = (codes_t, scales_t)
-            return (grouped,) + tuple(t[:, cols[0]:cols[1]] for t in made[kind, e, s])
-
-        def pack(job):
-            quantize(job[0][:], job[1], job[2])
+        def scatter(e, u, results, gate_sb):
+            first = (e * C + u * P) // LIST
+            for q in range(ROW_TILES):
+                nc.vector.tensor_tensor(placed[q][:].indirect(dst_sb[:, first:first + P // LIST]), results[q][:], gate_sb[:, u * P:(u + 1) * P], MULT)
 
         def load_gate(e):
-            nc.sync.dma_start(gate_sb[e][:], gate[:P, e * C:(e + 1) * C])
+            gate_sb = keep.tile([P, C], F32, name=f"gate{e}")
+            nc.sync.dma_start(gate_sb[:], gate[:P, e * C:(e + 1) * C])
+            return gate_sb
+
+        def whole_groups(first_bank, name):
+            return [(u, ALL, bank(first_bank + u, f"{name}{u}")) for u in range(SLOT_TILES)]
 
         for s in range(PASSES):
-            job = weave("x", 0, s)
+            raw = load_pass(xT, s)
             if s == 0:
                 nc.sync.dma_start(offs_sb[:], offs)
-            pack(job)
+            grouped = interleave(raw, VECTOR_COLUMNS["x", 0])
+            quantize(grouped[:], token_words[s][:], token_scales[s // PLANES][4 * (s % PLANES):P, :])
             for e in range(E):
-                gather_words(s, e)
-                if s >= 3:
-                    gather_bytes(s - 3, e)
-        for kind in ("w1", "w3"):
-            for s in range(PASSES):
-                job = weave(kind, 0, s)
-                if (kind, s) == ("w3", 0):
-                    sigmoids()
-                pack(job)
-                first_layer(kind, 0, s, WHOLE)
-        job = weave("w2", 0, 0, cols=(0, N))
-        nc.sync.dma_start(dst_sb[:], dst)
-        load_gate(0)
-        pack(job)
-        for u in range(2):
-            product(0, u, WHOLE)
-            turn(0, u)
+                gather(slot_words[s], token_words[s], e)
+                if s % PLANES == PLANES - 1 or s == PASSES - 1:
+                    gather(slot_scales[s // PLANES], token_scales[s // PLANES], e)
+
+        a_groups = whole_groups(A_BANK, "a")
         for s in range(PASSES):
-            job = weave("w1", 1, s)
-            if s == 0:
-                for u in range(2):
-                    quantize_hidden(0, u)
-                    second_layer(0, u)
-            if s in (1, 2):
-                for q in range(2):
-                    scatter(0, s - 1, q)
-            pack(job)
-            first_layer("w1", 1, s, WHOLE)
-        for s in range(LAST_PIECES[0][0]):
-            job = weave("w3", 1, s)
-            if s == 0:
-                sigmoids()
-            pack(job)
-            first_layer("w3", 1, s, WHOLE)
-        for s, cols, cut in LAST_PIECES[:-2]:
-            pack(weave("w3", 1, s, cols=cols, cut=cut))
-            first_layer("w3", 1, s, cols)
-        jobs = [weave("w3", 1, s, cols=cols, cut=cut) for s, cols, cut in LAST_PIECES[-2:]]
-        for job, (s, cols, cut) in zip(jobs, LAST_PIECES[-2:]):
-            pack(job)
-            first_layer("w3", 1, s, cols)
-        job = weave("w2", 1, 0, cols=(0, N))
-        load_gate(1)
-        product(1, 0, WHOLE)
-        turn(1, 0)
-        product(1, 1, WHOLE)
-        turn(1, 1)
-        pack(job)
-        for u in range(2):
-            quantize_hidden(1, u)
-            second_layer(1, u)
-        for u in range(2):
-            for q in range(2):
-                scatter(1, u, q)
-                if u == 1:
-                    nc.sync.dma_start(out[q * P:(q + 1) * P, :], placed[q][:])
+            first_layer_pass("w1", w1, 0, s, a_groups)
+        sig = sigmoids(a_groups)
+        b_groups = whole_groups(B_BANK, "b")
+        for s in range(PASSES):
+            first_layer_pass("w3", w3, 0, s, b_groups)
+
+        grouped = interleave(load_pass(w2[0], 0), VECTOR_COLUMNS["w2", 0])
+        nc.sync.dma_start(dst_sb[:], dst)
+        gate_sb = load_gate(0)
+        second = packed(N, "second")
+        quantize(grouped[:], second[0][:], second[1][:])
+        woven = [hidden_values(u, b_groups, sig) for u in range(SLOT_TILES)]
+        results = [second_layer(u, second, woven[u]) for u in range(SLOT_TILES)]
+        for u in range(SLOT_TILES):
+            scatter(0, u, results[u], gate_sb)
+
+        a_groups = whole_groups(A_BANK, "a")
+        for s in range(PASSES):
+            first_layer_pass("w1", w1, 1, s, a_groups)
+        sig = sigmoids(a_groups)
+        b_groups = [(u, columns, bank(B_BANK + g, f"b{g}")) for g, (u, columns) in enumerate(((0, LEFT), (0, RIGHT), (1, ALL)))]
+        for s in range(PASSES - 1):
+            first_layer_pass("w3", w3, 1, s, b_groups)
+
+        last_rows = w3[1][K - K_PASS:, :].rearrange("(p j) w -> p j w", j=PACK)
+        left, right = [work.tile([P, H // 2 * PACK], BF16, name=f"grouped{H // 2}", align_bytes=64) for side in range(2)]
+        for v, (to_left, to_right) in enumerate(((nc.scalar.copy, nc.vector.tensor_copy), (nc.vector.tensor_copy, nc.scalar.copy))):
+            rows = slice(2 * v, 2 * v + 2)
+            piece = keep.tile([P, 2, H], F32, name=f"piece{v}")
+            nc.sync.dma_start(piece[:], last_rows[:, rows, :])
+            weave(to_left, left, piece[:, :, LEFT], LEFT, rows)
+            weave(to_right, right, piece[:, :, RIGHT], LEFT, rows)
+        weights = packed(H, "weight")
+        for grouped, columns in ((left, LEFT), (right, RIGHT)):
+            quantize(grouped[:], weights[0][:, columns], weights[1][:, columns])
+        for u, columns, acc in b_groups:
+            multiply(acc, weights, 1, u, PASSES - 1, columns)
+
+        grouped = interleave(load_pass(w2[1], 0), VECTOR_COLUMNS["w2", 1])
+        gate_sb = load_gate(1)
+        woven = [hidden_values(u, b_groups, sig) for u in range(SLOT_TILES)]
+        second = packed(N, "second")
+        quantize(grouped[:], second[0][:], second[1][:])
+        results = [second_layer(u, second, woven[u]) for u in range(SLOT_TILES)]
+        for u in range(SLOT_TILES):
+            scatter(1, u, results[u], gate_sb)
+        for q in range(ROW_TILES):
+            nc.sync.dma_start(out[q * P:(q + 1) * P, :], placed[q][:])

@@ -24,10 +24,15 @@ SIGMOID = mybir.ActivationFunctionType.Sigmoid
 MULT = mybir.AluOpType.mult
 
 RUN = 2
+AHEAD = 5
+TWO_QUEUES = 0
 ALL = slice(0, H)
 LEFT, RIGHT = slice(0, H // 2), slice(H // 2, H)
 
-VECTOR_COLUMNS = {("x", 0): 64, ("w1", 0): 192, ("w3", 0): 256, ("w2", 0): 64, ("w1", 1): 128, ("w3", 1): 336, ("w2", 1): 0}
+VECTOR_COLUMNS = {("x", 0): 64, ("w1", 0): 192, ("w3", 0): 256, ("w2", 0): 64, ("w1", 1): 128, ("w3", 1): 224, ("w2", 1): 0}
+LAST_BUT_ONE = 320
+HELD = {}
+EARLY_SHARE = 256
 
 A_BANK, B_BANK, TURN_BANK = 0, 2, 6
 
@@ -55,20 +60,34 @@ def tile_moe_two_glu_sigmoid_kernel(tc, xT, w1, w3, w2, gate, offs, dst, out):
         slot_words = [keep.tile([P, E * C], U32, name=f"slot_words{s}", align_bytes=64) for s in range(PASSES)]
         placed = [keep.tile([P, T], F32, name=f"placed{q}") for q in range(ROW_TILES)]
 
-        def load_pass(matrix, s):
+        def load_pass(matrix, s, queue=nc.sync, ring=""):
             width = matrix.shape[1]
-            raw = stage.tile([P, PACK, width], F32, name=f"raw{width}", bufs=8 if width == H else E)
-            nc.sync.dma_start(raw[:], matrix[s * K_PASS:(s + 1) * K_PASS, :].rearrange("(p j) w -> p j w", j=PACK))
+            raw = stage.tile([P, PACK, width], F32, name=f"raw_{ring}", bufs=3)
+            queue.dma_start(raw[:], matrix[s * K_PASS:(s + 1) * K_PASS, :].rearrange("(p j) w -> p j w", j=PACK))
             return raw
+
+        stream = [(matrix, s) for matrix in (xT, w1[0], w3[0], w1[1], w3[1]) for s in range(PASSES)]
+        landed = []
+
+        def fetch(upto):
+            for n in range(len(landed), min(upto, len(stream))):
+                landed.append(load_pass(*stream[n], nc.scalar if n % 2 and n < TWO_QUEUES else nc.sync, "odd" if n % 2 else "even"))
+
+        def take(n):
+            fetch(min(n + 1 + AHEAD, 3 * PASSES) if n < 3 * PASSES else n + 1)
+            return landed[n]
 
         def weave(copy, grouped, raw, columns, rows):
             runs = slice(columns.start // RUN, columns.stop // RUN)
             to = grouped[:].rearrange("p (c i j) -> p c j i", i=RUN, j=PACK)
             copy(to[:, runs, rows], raw[:].rearrange("p j (c i) -> p c j i", i=RUN)[:, runs])
 
-        def interleave(raw, cut):
+        def interleave(raw, cut, held=None):
             width = raw.shape[2]
-            grouped = work.tile([P, width * PACK], BF16, name=f"grouped{width}", align_bytes=64)
+            if held:
+                grouped = keep.tile([P, width * PACK], BF16, name="held_grouped", tag=held, align_bytes=64)
+            else:
+                grouped = work.tile([P, width * PACK], BF16, name=f"grouped{width}", align_bytes=64)
             if cut > 0:
                 weave(nc.vector.tensor_copy, grouped, raw, slice(0, cut), slice(0, PACK))
             weave(nc.scalar.copy, grouped, raw, slice(cut, width), slice(0, PACK))
@@ -102,7 +121,8 @@ def tile_moe_two_glu_sigmoid_kernel(tc, xT, w1, w3, w2, gate, offs, dst, out):
             )
 
         def first_layer_pass(name, matrix, e, s, groups):
-            grouped = interleave(load_pass(matrix[e], s), VECTOR_COLUMNS[name, e])
+            raw = take(PASSES * (2 * e + (1 if name == "w1" else 2)) + s)
+            grouped = interleave(raw, LAST_BUT_ONE if (name, e, s) == ("w3", 1, PASSES - 2) else EARLY_SHARE if (name, e) == ("w1", 1) and s < 2 else VECTOR_COLUMNS[name, e], HELD.get((name, e, s)))
             weights = packed(H, "weight")
             quantize(grouped[:], weights[0][:], weights[1][:])
             for u, columns, acc in groups:
@@ -111,10 +131,11 @@ def tile_moe_two_glu_sigmoid_kernel(tc, xT, w1, w3, w2, gate, offs, dst, out):
         def by_pair(columns):
             return columns.rearrange("s (p w r) -> s w p r", w=2, r=2)
 
-        def sigmoids(groups):
-            sig = [keep.tile([P, 2, P, 2], F32, name=f"sig{u}") for u in range(SLOT_TILES)]
+        def sigmoids(e, groups):
+            both = keep.tile([P, SLOT_TILES, 2, P, 2], F32, name="sig", tag=f"sig{e}", align_bytes=64)
+            sig = [both[:, u] for u in range(SLOT_TILES)]
             for u, columns, acc in groups:
-                nc.scalar.activation(sig[u][:], by_pair(acc[:, columns]), SIGMOID)
+                nc.scalar.activation(sig[u], by_pair(acc[:, columns]), SIGMOID)
             return sig
 
         def hidden_values(u, groups, sig):
@@ -156,20 +177,28 @@ def tile_moe_two_glu_sigmoid_kernel(tc, xT, w1, w3, w2, gate, offs, dst, out):
         def scatter(e, u, results, gate_sb):
             first = (e * C + u * P) // LIST
             for q in range(ROW_TILES):
-                nc.vector.tensor_tensor(placed[q][:].indirect(dst_sb[:, first:first + P // LIST]), results[q][:], gate_sb[:, u * P:(u + 1) * P], MULT)
+                nc.vector.tensor_tensor(placed[q][:].indirect(dst_sb[:, first:first + P // LIST]), results[q][:], gate_sb[:, e * C + u * P:e * C + (u + 1) * P], MULT)
 
-        def load_gate(e):
-            gate_sb = keep.tile([P, C], F32, name=f"gate{e}")
-            nc.sync.dma_start(gate_sb[:], gate[:P, e * C:(e + 1) * C])
+        def spread_gate():
+            share = E * C // P
+            column = keep.tile([P, share], F32, name="gate_column")
+            nc.sync.dma_start(column[:], gate[0].rearrange("(p c) -> p c", c=share))
+            spread = bank(TURN_BANK, "spread")
+            for c in range(share):
+                nc.tensor.transpose(spread[:, c * P:(c + 1) * P], column[:, c:c + 1].to_broadcast([P, P]), identity[:])
+            gate_sb = keep.tile([P, E * C], F32, name="gate_sb")
+            nc.scalar.copy(gate_sb[:].rearrange("m (p c) -> m p c", c=share), spread[:].rearrange("m (c p) -> m p c", c=share))
             return gate_sb
 
         def whole_groups(first_bank, name):
             return [(u, ALL, bank(first_bank + u, f"{name}{u}")) for u in range(SLOT_TILES)]
 
         for s in range(PASSES):
-            raw = load_pass(xT, s)
             if s == 0:
+                fetch(1)
                 nc.sync.dma_start(offs_sb[:], offs)
+                gate_sb = spread_gate()
+            raw = take(s)
             grouped = interleave(raw, VECTOR_COLUMNS["x", 0])
             quantize(grouped[:], token_words[s][:], token_scales[s // PLANES][4 * (s % PLANES):P, :])
             for e in range(E):
@@ -180,34 +209,36 @@ def tile_moe_two_glu_sigmoid_kernel(tc, xT, w1, w3, w2, gate, offs, dst, out):
         a_groups = whole_groups(A_BANK, "a")
         for s in range(PASSES):
             first_layer_pass("w1", w1, 0, s, a_groups)
-        sig = sigmoids(a_groups)
+        sig = sigmoids(0, a_groups)
         b_groups = whole_groups(B_BANK, "b")
         for s in range(PASSES):
             first_layer_pass("w3", w3, 0, s, b_groups)
 
-        grouped = interleave(load_pass(w2[0], 0), VECTOR_COLUMNS["w2", 0])
+        grouped = interleave(load_pass(w2[0], 0, ring="odd"), VECTOR_COLUMNS["w2", 0])
         nc.sync.dma_start(dst_sb[:], dst)
-        gate_sb = load_gate(0)
         second = packed(N, "second")
         quantize(grouped[:], second[0][:], second[1][:])
-        woven = [hidden_values(u, b_groups, sig) for u in range(SLOT_TILES)]
-        results = [second_layer(u, second, woven[u]) for u in range(SLOT_TILES)]
-        for u in range(SLOT_TILES):
-            scatter(0, u, results[u], gate_sb)
 
         a_groups = whole_groups(A_BANK, "a")
         for s in range(PASSES):
             first_layer_pass("w1", w1, 1, s, a_groups)
-        sig = sigmoids(a_groups)
+            if s == 0:
+                woven = [hidden_values(u, b_groups, sig) for u in range(SLOT_TILES)]
+            if s == 1:
+                results = [second_layer(u, second, woven[u]) for u in range(SLOT_TILES)]
+                for u in range(SLOT_TILES):
+                    scatter(0, u, results[u], gate_sb)
         b_groups = [(u, columns, bank(B_BANK + g, f"b{g}")) for g, (u, columns) in enumerate(((0, LEFT), (0, RIGHT), (1, ALL)))]
         for s in range(PASSES - 1):
             first_layer_pass("w3", w3, 1, s, b_groups)
+            if s == 1:
+                sig = sigmoids(1, a_groups)
 
         last_rows = w3[1][K - K_PASS:, :].rearrange("(p j) w -> p j w", j=PACK)
         left, right = [work.tile([P, H // 2 * PACK], BF16, name=f"grouped{H // 2}", align_bytes=64) for side in range(2)]
         for v, (to_left, to_right) in enumerate(((nc.scalar.copy, nc.vector.tensor_copy), (nc.vector.tensor_copy, nc.scalar.copy))):
             rows = slice(2 * v, 2 * v + 2)
-            piece = keep.tile([P, 2, H], F32, name=f"piece{v}")
+            piece = stage.tile([P, 2, H], F32, name="raw_odd" if v else "raw_even", bufs=3)
             nc.sync.dma_start(piece[:], last_rows[:, rows, :])
             weave(to_left, left, piece[:, :, LEFT], LEFT, rows)
             weave(to_right, right, piece[:, :, RIGHT], LEFT, rows)
@@ -217,8 +248,7 @@ def tile_moe_two_glu_sigmoid_kernel(tc, xT, w1, w3, w2, gate, offs, dst, out):
         for u, columns, acc in b_groups:
             multiply(acc, weights, 1, u, PASSES - 1, columns)
 
-        grouped = interleave(load_pass(w2[1], 0), VECTOR_COLUMNS["w2", 1])
-        gate_sb = load_gate(1)
+        grouped = interleave(load_pass(w2[1], 0, ring="odd"), VECTOR_COLUMNS["w2", 1])
         woven = [hidden_values(u, b_groups, sig) for u in range(SLOT_TILES)]
         second = packed(N, "second")
         quantize(grouped[:], second[0][:], second[1][:])

@@ -138,7 +138,7 @@ def tile_moe_two_glu_sigmoid_kernel(tc, xT, w1, w3, w2, gate, offs, dst, out):
                 nc.scalar.activation(sig[u], by_pair(acc[:, columns]), SIGMOID)
             return sig
 
-        def hidden_values(u, groups, sig):
+        def hidden_values(u, groups, sig, copy=nc.scalar.copy):
             hidden = keep.tile([P, 2, P, 2], BF16, name=f"hidden{u}")
             for tile, columns, acc in groups:
                 if tile == u:
@@ -149,7 +149,7 @@ def tile_moe_two_glu_sigmoid_kernel(tc, xT, w1, w3, w2, gate, offs, dst, out):
             for w in range(2):
                 nc.tensor.transpose(turned[:, w * P:(w + 1) * P], pairs[:, w * P:(w + 1) * P], identity[:])
             woven = keep.tile([P, P * PACK], BF16, name=f"woven{u}", align_bytes=64)
-            nc.scalar.copy(woven[:].bitcast(F32).rearrange("p (c w) -> p c w", w=2), turned[:, :2 * P].rearrange("p (w c) -> p c w", w=2))
+            copy(woven[:].bitcast(F32).rearrange("p (c w) -> p c w", w=2), turned[:, :2 * P].rearrange("p (w c) -> p c w", w=2))
             return woven
 
         def second_layer(u, weights, woven):
@@ -181,13 +181,19 @@ def tile_moe_two_glu_sigmoid_kernel(tc, xT, w1, w3, w2, gate, offs, dst, out):
 
         def spread_gate():
             share = E * C // P
+            row = keep.tile([P, E * C], F32, name="gate_row")
+            nc.vector.memset(row[:P - 1, :], 0.0)
+            nc.scalar.dma_start(row[P - 1:, :], gate[0:1, :])
+            upright = bank(TURN_BANK + 1, "upright")
+            for c in range(share):
+                nc.tensor.transpose(upright[:, c * P:(c + 1) * P], row[:, c * P:(c + 1) * P], identity[:])
             column = keep.tile([P, share], F32, name="gate_column")
-            nc.sync.dma_start(column[:], gate[0].rearrange("(p c) -> p c", c=share))
+            nc.scalar.copy(column[:], upright[:, P - 1::P])
             spread = bank(TURN_BANK, "spread")
             for c in range(share):
                 nc.tensor.transpose(spread[:, c * P:(c + 1) * P], column[:, c:c + 1].to_broadcast([P, P]), identity[:])
             gate_sb = keep.tile([P, E * C], F32, name="gate_sb")
-            nc.scalar.copy(gate_sb[:].rearrange("m (p c) -> m p c", c=share), spread[:].rearrange("m (c p) -> m p c", c=share))
+            nc.scalar.copy(gate_sb[:], spread[:])
             return gate_sb
 
         def whole_groups(first_bank, name):
@@ -249,7 +255,7 @@ def tile_moe_two_glu_sigmoid_kernel(tc, xT, w1, w3, w2, gate, offs, dst, out):
             multiply(acc, weights, 1, u, PASSES - 1, columns)
 
         grouped = interleave(load_pass(w2[1], 0, ring="odd"), VECTOR_COLUMNS["w2", 1])
-        woven = [hidden_values(u, b_groups, sig) for u in range(SLOT_TILES)]
+        woven = [hidden_values(u, b_groups, sig, copy) for u, copy in enumerate((nc.scalar.copy, nc.scalar.copy))]
         second = packed(N, "second")
         quantize(grouped[:], second[0][:], second[1][:])
         results = [second_layer(u, second, woven[u]) for u in range(SLOT_TILES)]

@@ -58,11 +58,11 @@ def tile_moe_two_glu_sigmoid_kernel(tc, xT, w1, w3, w2, gate, offs, dst, out):
         make_identity(nc, identity[:])
         token_words = [keep.tile([P, T], U32, name=f"token_words{s}", align_bytes=64) for s in range(PASSES)]
         slot_words = [keep.tile([P, E * C], U32, name=f"slot_words{s}", align_bytes=64) for s in range(PASSES)]
-        placed = [keep.tile([P, T], F32, name=f"placed{q}") for q in range(ROW_TILES)]
+        placed = [keep.tile([P, T], F32, name=f"placed{q}", align_bytes=256) for q in range(ROW_TILES)]
 
         def load_pass(matrix, s, queue=nc.sync, ring=""):
             width = matrix.shape[1]
-            raw = stage.tile([P, PACK, width], F32, name=f"raw_{ring}", bufs=3)
+            raw = stage.tile([P, PACK, width], F32, name=f"raw_{ring}", bufs=3, align_bytes=256)
             queue.dma_start(raw[:], matrix[s * K_PASS:(s + 1) * K_PASS, :].rearrange("(p j) w -> p j w", j=PACK))
             return raw
 
@@ -244,7 +244,7 @@ def tile_moe_two_glu_sigmoid_kernel(tc, xT, w1, w3, w2, gate, offs, dst, out):
         left, right = [work.tile([P, H // 2 * PACK], BF16, name=f"grouped{H // 2}", align_bytes=64) for side in range(2)]
         for v, (to_left, to_right) in enumerate(((nc.scalar.copy, nc.vector.tensor_copy), (nc.vector.tensor_copy, nc.scalar.copy))):
             rows = slice(2 * v, 2 * v + 2)
-            piece = stage.tile([P, 2, H], F32, name="raw_odd" if v else "raw_even", bufs=3)
+            piece = stage.tile([P, 2, H], F32, name="raw_odd" if v else "raw_even", bufs=3, align_bytes=256)
             nc.sync.dma_start(piece[:], last_rows[:, rows, :])
             weave(to_left, left, piece[:, :, LEFT], LEFT, rows)
             weave(to_right, right, piece[:, :, RIGHT], LEFT, rows)

@@ -24,17 +24,12 @@ SIGMOID = mybir.ActivationFunctionType.Sigmoid
 MULT = mybir.AluOpType.mult
 
 RUN = 2
-AHEAD = 5
-TWO_QUEUES = 0
-ALL = slice(0, H)
-LEFT, RIGHT = slice(0, H // 2), slice(H // 2, H)
 
-VECTOR_COLUMNS = {("x", 0): 64, ("w1", 0): 192, ("w3", 0): 256, ("w2", 0): 64, ("w1", 1): 128, ("w3", 1): 224, ("w2", 1): 0}
-LAST_BUT_ONE = 320
-HELD = {}
-EARLY_SHARE = 256
+VECTOR_COLUMNS = {("x", 0): 64, ("w1", 0): 192, ("w3", 0): 256, ("w2", 0): 64, ("w1", 1): 160, ("w3", 1): 256}
 
-A_BANK, B_BANK, TURN_BANK = 0, 2, 6
+PIECES = ((128, 128), (64, 64, 128))
+
+A_BANK, B_BANK, Y_BANK = 0, 2, 4
 
 
 def tile_moe_two_glu_sigmoid_kernel(tc, xT, w1, w3, w2, gate, offs, dst, out):
@@ -60,37 +55,30 @@ def tile_moe_two_glu_sigmoid_kernel(tc, xT, w1, w3, w2, gate, offs, dst, out):
         slot_words = [keep.tile([P, E * C], U32, name=f"slot_words{s}", align_bytes=64) for s in range(PASSES)]
         placed = [keep.tile([P, T], F32, name=f"placed{q}", align_bytes=256) for q in range(ROW_TILES)]
 
-        def load_pass(matrix, s, queue=nc.sync, ring=""):
-            width = matrix.shape[1]
-            raw = stage.tile([P, PACK, width], F32, name=f"raw_{ring}", bufs=3, align_bytes=256)
-            queue.dma_start(raw[:], matrix[s * K_PASS:(s + 1) * K_PASS, :].rearrange("(p j) w -> p j w", j=PACK))
+        def load(matrix, s, rows=slice(0, PACK)):
+            raw = stage.tile([P, rows.stop - rows.start, matrix.shape[1]], F32, name="raw", align_bytes=256)
+            nc.sync.dma_start(raw[:], matrix[s * K_PASS:(s + 1) * K_PASS, :].rearrange("(p j) w -> p j w", j=PACK)[:, rows, :])
             return raw
 
-        stream = [(matrix, s) for matrix in (xT, w1[0], w3[0], w1[1], w3[1]) for s in range(PASSES)]
-        landed = []
+        def values_tile(width):
+            return work.tile([P, width * PACK], BF16, name=f"grouped{width}", align_bytes=64)
 
-        def fetch(upto):
-            for n in range(len(landed), min(upto, len(stream))):
-                landed.append(load_pass(*stream[n], nc.scalar if n % 2 and n < TWO_QUEUES else nc.sync, "odd" if n % 2 else "even"))
+        def weave(copy, grouped, raw):
+            copy(grouped.rearrange("p (c i j) -> p c j i", i=RUN, j=PACK), raw.rearrange("p j (c i) -> p c j i", i=RUN))
 
-        def take(n):
-            fetch(min(n + 1 + AHEAD, 3 * PASSES) if n < 3 * PASSES else n + 1)
-            return landed[n]
-
-        def weave(copy, grouped, raw, columns, rows):
-            runs = slice(columns.start // RUN, columns.stop // RUN)
-            to = grouped[:].rearrange("p (c i j) -> p c j i", i=RUN, j=PACK)
-            copy(to[:, runs, rows], raw[:].rearrange("p j (c i) -> p c j i", i=RUN)[:, runs])
-
-        def interleave(raw, cut, held=None):
+        def interleave(raw, cut):
             width = raw.shape[2]
-            if held:
-                grouped = keep.tile([P, width * PACK], BF16, name="held_grouped", tag=held, align_bytes=64)
-            else:
-                grouped = work.tile([P, width * PACK], BF16, name=f"grouped{width}", align_bytes=64)
-            if cut > 0:
-                weave(nc.vector.tensor_copy, grouped, raw, slice(0, cut), slice(0, PACK))
-            weave(nc.scalar.copy, grouped, raw, slice(cut, width), slice(0, PACK))
+            grouped = values_tile(width)
+            weave(nc.vector.tensor_copy, grouped[:, :cut * PACK], raw[:, :, :cut])
+            weave(nc.scalar.copy, grouped[:, cut * PACK:], raw[:, :, cut:])
+            return grouped
+
+        def interleave_in_quarters(raw, cut):
+            grouped = values_tile(H)
+            to = grouped[:].rearrange("p (t m j) -> p m j t", t=PACK, j=PACK)
+            source = raw[:].rearrange("p j (m t) -> p m j t", t=PACK)
+            nc.vector.tensor_copy(to[:, :cut // PACK], source[:, :cut // PACK])
+            nc.scalar.copy(to[:, cut // PACK:], source[:, cut // PACK:])
             return grouped
 
         def quantize(values, codes, scales):
@@ -101,110 +89,109 @@ def tile_moe_two_glu_sigmoid_kernel(tc, xT, w1, w3, w2, gate, offs, dst, out):
             scales = work.tile([P, width], U8, name=f"{name}_scales", align_bytes=64)
             return codes, scales
 
+        def quantized(values, name):
+            codes, scales = packed(values.shape[1] // PACK, name)
+            quantize(values, codes[:], scales[:])
+            return codes, scales
+
         def bank(b, name):
             return psum.tile([P, 512], F32, tag=f"bank{b}", name=name)
 
         def gather(slots, tokens, e):
             nc.vector.tensor_copy(slots[:, e * C:(e + 1) * C], tokens[:].indirect(offs_sb[:, e * C // LIST:(e + 1) * C // LIST]))
 
-        def multiply(acc, weights, e, u, s, columns):
+        def multiply(acc, weights, first, e, u, s, t):
             codes, scales = weights
             slots = slice(e * C + u * P, e * C + (u + 1) * P)
             nc.tensor.matmul_mx(
-                out=acc[:, :columns.stop - columns.start],
-                lhsT=slot_words[s][:, slots].bitcast(FP8X4),
-                lhsT_scale=slot_scales[s // PLANES][4 * (s % PLANES):P, slots],
-                rhs=codes[:, columns].bitcast(FP8X4),
-                rhs_scale=scales[:, columns],
-                start=(s == 0),
-                stop=(s == PASSES - 1),
+                out=acc[:, t * P:(t + 1) * P],
+                lhsT=codes[:, first:first + P].bitcast(FP8X4),
+                lhsT_scale=scales[:, first:first + P],
+                rhs=slot_words[s][:, slots].bitcast(FP8X4),
+                rhs_scale=slot_scales[s // PLANES][4 * (s % PLANES):P, slots],
+                start=(s == 0 and t == 0),
+                stop=(s == PASSES - 1 and t == PACK - 1),
             )
 
-        def first_layer_pass(name, matrix, e, s, groups):
-            raw = take(PASSES * (2 * e + (1 if name == "w1" else 2)) + s)
-            grouped = interleave(raw, LAST_BUT_ONE if (name, e, s) == ("w3", 1, PASSES - 2) else EARLY_SHARE if (name, e) == ("w1", 1) and s < 2 else VECTOR_COLUMNS[name, e], HELD.get((name, e, s)))
-            weights = packed(H, "weight")
-            quantize(grouped[:], weights[0][:], weights[1][:])
-            for u, columns, acc in groups:
-                multiply(acc, weights, e, u, s, columns)
+        def first_layer_pass(name, matrix, e, s, banks):
+            weights = quantized(interleave_in_quarters(load(matrix[e], s), VECTOR_COLUMNS[name, e])[:], "weight")
+            for t in range(PACK):
+                for u in range(SLOT_TILES):
+                    multiply(banks[u], weights, t * P, e, u, s, t)
 
-        def by_pair(columns):
-            return columns.rearrange("s (p w r) -> s w p r", w=2, r=2)
+        def by_slot(acc):
+            return acc[:].rearrange("p (t c) -> p c t", t=PACK)
 
-        def sigmoids(e, groups):
-            both = keep.tile([P, SLOT_TILES, 2, P, 2], F32, name="sig", tag=f"sig{e}", align_bytes=64)
-            sig = [both[:, u] for u in range(SLOT_TILES)]
-            for u, columns, acc in groups:
-                nc.scalar.activation(sig[u], by_pair(acc[:, columns]), SIGMOID)
+        def sigmoids(e, banks):
+            sig = keep.tile([P, C, PACK], F32, name=f"sig{e}", align_bytes=64)
+            for u in range(SLOT_TILES):
+                nc.scalar.activation(sig[:, u * P:(u + 1) * P], by_slot(banks[u]), SIGMOID)
             return sig
 
-        def hidden_values(u, groups, sig, copy=nc.scalar.copy):
-            hidden = keep.tile([P, 2, P, 2], BF16, name=f"hidden{u}")
-            for tile, columns, acc in groups:
-                if tile == u:
-                    words = slice(columns.start // PACK, columns.stop // PACK)
-                    nc.vector.tensor_tensor(hidden[:, :, words], by_pair(acc[:, :columns.stop - columns.start]), sig[u][:, :, words], MULT)
-            pairs = hidden[:].rearrange("s w p r -> s (w p r)").bitcast(F32)
-            turned = bank(TURN_BANK + u, f"turned{u}")
-            for w in range(2):
-                nc.tensor.transpose(turned[:, w * P:(w + 1) * P], pairs[:, w * P:(w + 1) * P], identity[:])
-            woven = keep.tile([P, P * PACK], BF16, name=f"woven{u}", align_bytes=64)
-            copy(woven[:].bitcast(F32).rearrange("p (c w) -> p c w", w=2), turned[:, :2 * P].rearrange("p (w c) -> p c w", w=2))
-            return woven
+        def pieces(e):
+            return [slice(sum(PIECES[e][:r]), sum(PIECES[e][:r + 1])) for r in range(len(PIECES[e]))]
 
-        def second_layer(u, weights, woven):
-            codes, scales = weights
-            h_codes, h_scales = packed(P, "hidden")
-            quantize(woven[:], h_codes[:], h_scales[:])
-            results = []
-            for q in range(ROW_TILES):
-                rows = slice(q * P, (q + 1) * P)
-                y = bank(B_BANK + ROW_TILES * u + q, f"y{u}{q}")
+        def hidden_values(e, piece, banks, sig):
+            count = piece.stop - piece.start
+            hidden = keep.tile([P, count * PACK], BF16, name=f"hidden{e}_{piece.start}", align_bytes=64)
+            inside = slice(piece.start % P, piece.start % P + count)
+            nc.vector.tensor_tensor(hidden[:].rearrange("p (c t) -> p c t", t=PACK), by_slot(banks[piece.start // P])[:, inside], sig[:, piece], MULT)
+            return hidden
+
+        def second_layer(e, r, second, moving):
+            h_codes, h_scales = moving
+            count = PIECES[e][r]
+            y = bank(Y_BANK + r, f"y{e}{r}")
+            for q, (codes, scales) in enumerate(second):
                 nc.tensor.matmul_mx(
-                    out=y[:, :P],
-                    lhsT=codes[:, rows].bitcast(FP8X4),
-                    lhsT_scale=scales[:, rows],
+                    out=y[:, q * count:(q + 1) * count],
+                    lhsT=codes.bitcast(FP8X4),
+                    lhsT_scale=scales,
                     rhs=h_codes[:].bitcast(FP8X4),
                     rhs_scale=h_scales[:],
                     start=True,
                     stop=True,
                 )
-                result = keep.tile([P, P], F32, name=f"result{u}{q}")
-                nc.scalar.copy(result[:], y[:, :P])
-                results.append(result)
-            return results
+            result = keep.tile([P, ROW_TILES * count], F32, name=f"result{e}{r}")
+            nc.scalar.copy(result[:], y[:, :ROW_TILES * count])
+            return result
 
-        def scatter(e, u, results, gate_sb):
-            first = (e * C + u * P) // LIST
+        def scatter(e, piece, result, gate_sb):
+            count = piece.stop - piece.start
+            first = e * C + piece.start
             for q in range(ROW_TILES):
-                nc.vector.tensor_tensor(placed[q][:].indirect(dst_sb[:, first:first + P // LIST]), results[q][:], gate_sb[:, e * C + u * P:e * C + (u + 1) * P], MULT)
+                nc.vector.tensor_tensor(
+                    placed[q][:].indirect(dst_sb[:, first // LIST:(first + count) // LIST]),
+                    result[:, q * count:(q + 1) * count],
+                    gate_sb[:, first:first + count],
+                    MULT,
+                )
 
         def spread_gate():
             share = E * C // P
             row = keep.tile([P, E * C], F32, name="gate_row")
             nc.vector.memset(row[:P - 1, :], 0.0)
             nc.scalar.dma_start(row[P - 1:, :], gate[0:1, :])
-            upright = bank(TURN_BANK + 1, "upright")
+            upright = bank(Y_BANK + 1, "upright")
             for c in range(share):
                 nc.tensor.transpose(upright[:, c * P:(c + 1) * P], row[:, c * P:(c + 1) * P], identity[:])
             column = keep.tile([P, share], F32, name="gate_column")
             nc.scalar.copy(column[:], upright[:, P - 1::P])
-            spread = bank(TURN_BANK, "spread")
+            spread = bank(Y_BANK, "spread")
             for c in range(share):
                 nc.tensor.transpose(spread[:, c * P:(c + 1) * P], column[:, c:c + 1].to_broadcast([P, P]), identity[:])
             gate_sb = keep.tile([P, E * C], F32, name="gate_sb")
             nc.scalar.copy(gate_sb[:], spread[:])
             return gate_sb
 
-        def whole_groups(first_bank, name):
-            return [(u, ALL, bank(first_bank + u, f"{name}{u}")) for u in range(SLOT_TILES)]
+        def banks_of(first_bank, name):
+            return [bank(first_bank + u, f"{name}{u}") for u in range(SLOT_TILES)]
 
         for s in range(PASSES):
+            raw = load(xT, s)
             if s == 0:
-                fetch(1)
                 nc.sync.dma_start(offs_sb[:], offs)
                 gate_sb = spread_gate()
-            raw = take(s)
             grouped = interleave(raw, VECTOR_COLUMNS["x", 0])
             quantize(grouped[:], token_words[s][:], token_scales[s // PLANES][4 * (s % PLANES):P, :])
             for e in range(E):
@@ -212,54 +199,53 @@ def tile_moe_two_glu_sigmoid_kernel(tc, xT, w1, w3, w2, gate, offs, dst, out):
                 if s % PLANES == PLANES - 1 or s == PASSES - 1:
                     gather(slot_scales[s // PLANES], token_scales[s // PLANES], e)
 
-        a_groups = whole_groups(A_BANK, "a")
+        a_banks = banks_of(A_BANK, "a")
         for s in range(PASSES):
-            first_layer_pass("w1", w1, 0, s, a_groups)
-        sig = sigmoids(0, a_groups)
-        b_groups = whole_groups(B_BANK, "b")
+            first_layer_pass("w1", w1, 0, s, a_banks)
+        sig = sigmoids(0, a_banks)
+        b_banks = banks_of(B_BANK, "b")
         for s in range(PASSES):
-            first_layer_pass("w3", w3, 0, s, b_groups)
-
-        grouped = interleave(load_pass(w2[0], 0, ring="odd"), VECTOR_COLUMNS["w2", 0])
+            first_layer_pass("w3", w3, 0, s, b_banks)
+        codes, scales = quantized(interleave(load(w2[0], 0), VECTOR_COLUMNS["w2", 0])[:], "second")
+        second = [(codes[:, q * P:(q + 1) * P], scales[:, q * P:(q + 1) * P]) for q in range(ROW_TILES)]
         nc.sync.dma_start(dst_sb[:], dst)
-        second = packed(N, "second")
-        quantize(grouped[:], second[0][:], second[1][:])
 
-        a_groups = whole_groups(A_BANK, "a")
+        a_banks = banks_of(A_BANK, "a")
         for s in range(PASSES):
-            first_layer_pass("w1", w1, 1, s, a_groups)
+            first_layer_pass("w1", w1, 1, s, a_banks)
             if s == 0:
-                woven = [hidden_values(u, b_groups, sig) for u in range(SLOT_TILES)]
-            if s == 1:
-                results = [second_layer(u, second, woven[u]) for u in range(SLOT_TILES)]
-                for u in range(SLOT_TILES):
-                    scatter(0, u, results[u], gate_sb)
-        b_groups = [(u, columns, bank(B_BANK + g, f"b{g}")) for g, (u, columns) in enumerate(((0, LEFT), (0, RIGHT), (1, ALL)))]
+                hidden = [hidden_values(0, piece, b_banks, sig) for piece in pieces(0)]
+                results = [second_layer(0, r, second, quantized(values[:], "hidden")) for r, values in enumerate(hidden)]
+            if s in (1, 2):
+                scatter(0, pieces(0)[s - 1], results[s - 1], gate_sb)
+        b_banks = banks_of(B_BANK, "b")
         for s in range(PASSES - 1):
-            first_layer_pass("w3", w3, 1, s, b_groups)
+            first_layer_pass("w3", w3, 1, s, b_banks)
             if s == 1:
-                sig = sigmoids(1, a_groups)
+                sig = sigmoids(1, a_banks)
 
-        last_rows = w3[1][K - K_PASS:, :].rearrange("(p j) w -> p j w", j=PACK)
-        left, right = [work.tile([P, H // 2 * PACK], BF16, name=f"grouped{H // 2}", align_bytes=64) for side in range(2)]
-        for v, (to_left, to_right) in enumerate(((nc.scalar.copy, nc.vector.tensor_copy), (nc.vector.tensor_copy, nc.scalar.copy))):
+        halves = [values_tile(H // 2) for side in range(2)]
+        for v in range(2):
             rows = slice(2 * v, 2 * v + 2)
-            piece = stage.tile([P, 2, H], F32, name="raw_odd" if v else "raw_even", bufs=3, align_bytes=256)
-            nc.sync.dma_start(piece[:], last_rows[:, rows, :])
-            weave(to_left, left, piece[:, :, LEFT], LEFT, rows)
-            weave(to_right, right, piece[:, :, RIGHT], LEFT, rows)
-        weights = packed(H, "weight")
-        for grouped, columns in ((left, LEFT), (right, RIGHT)):
-            quantize(grouped[:], weights[0][:, columns], weights[1][:, columns])
-        for u, columns, acc in b_groups:
-            multiply(acc, weights, 1, u, PASSES - 1, columns)
+            source = load(w3[1], PASSES - 1, rows)[:].rearrange("p j (m t) -> p m j t", t=PACK)
+            for side, copy in enumerate((nc.vector.tensor_copy, nc.scalar.copy)):
+                copy(halves[side][:].rearrange("p (t m j) -> p m j t", t=2, j=PACK)[:, :, rows], source[:, :, :, 2 * side:2 * side + 2])
+        weights = [quantized(values[:], "last") for values in halves]
+        for side in range(2):
+            for u in range(SLOT_TILES):
+                for t in range(2):
+                    multiply(b_banks[u], weights[side], t * P, 1, u, PASSES - 1, 2 * side + t)
 
-        grouped = interleave(load_pass(w2[1], 0, ring="odd"), VECTOR_COLUMNS["w2", 1])
-        woven = [hidden_values(u, b_groups, sig, copy) for u, copy in enumerate((nc.scalar.copy, nc.scalar.copy))]
-        second = packed(N, "second")
-        quantize(grouped[:], second[0][:], second[1][:])
-        results = [second_layer(u, second, woven[u]) for u in range(SLOT_TILES)]
-        for u in range(SLOT_TILES):
-            scatter(1, u, results[u], gate_sb)
+        raw = load(w2[1], 0)
+        columns = [values_tile(P) for q in range(ROW_TILES)]
+        for q, copy in enumerate((nc.vector.tensor_copy, nc.scalar.copy)):
+            weave(copy, columns[q][:], raw[:, :, q * P:(q + 1) * P])
+        hidden = [hidden_values(1, pieces(1)[0], b_banks, sig)]
+        second = [[part[:] for part in quantized(values[:], "second_half")] for values in columns]
+        results = [second_layer(1, 0, second, quantized(hidden[0][:], "hidden"))]
+        hidden.extend(hidden_values(1, piece, b_banks, sig) for piece in pieces(1)[1:])
+        results.extend(second_layer(1, r, second, quantized(hidden[r][:], "hidden")) for r in range(1, len(hidden)))
+        for piece, result in zip(pieces(1), results):
+            scatter(1, piece, result, gate_sb)
         for q in range(ROW_TILES):
             nc.sync.dma_start(out[q * P:(q + 1) * P, :], placed[q][:])

@@ -25,11 +25,11 @@ MULT = mybir.AluOpType.mult
 
 RUN = 2
 
-VECTOR_COLUMNS = {("x", 0): 64, ("w1", 0): 192, ("w3", 0): 256, ("w2", 0): 64, ("w1", 1): 160, ("w3", 1): 256}
+VECTOR_COLUMNS = {("x", 0): 64, ("w1", 0): 192, ("w3", 0): 256, ("w2", 0): 64, ("w1", 1): 192, ("w3", 1): 256}
 
-PIECES = ((128, 128), (64, 64, 128))
+PIECES = (slice(0, 64), slice(64, 128), slice(128, 256))
 
-A_BANK, B_BANK, Y_BANK = 0, 2, 4
+A_BANK, B_BANK, Y_BANK, TURN_BANK = 0, 2, 4, 6
 
 
 def tile_moe_two_glu_sigmoid_kernel(tc, xT, w1, w3, w2, gate, offs, dst, out):
@@ -100,84 +100,89 @@ def tile_moe_two_glu_sigmoid_kernel(tc, xT, w1, w3, w2, gate, offs, dst, out):
         def gather(slots, tokens, e):
             nc.vector.tensor_copy(slots[:, e * C:(e + 1) * C], tokens[:].indirect(offs_sb[:, e * C // LIST:(e + 1) * C // LIST]))
 
-        def multiply(acc, weights, first, e, u, s, t):
-            codes, scales = weights
-            slots = slice(e * C + u * P, e * C + (u + 1) * P)
+        def product(acc, stationary, moving, start, stop):
             nc.tensor.matmul_mx(
-                out=acc[:, t * P:(t + 1) * P],
-                lhsT=codes[:, first:first + P].bitcast(FP8X4),
-                lhsT_scale=scales[:, first:first + P],
-                rhs=slot_words[s][:, slots].bitcast(FP8X4),
-                rhs_scale=slot_scales[s // PLANES][4 * (s % PLANES):P, slots],
-                start=(s == 0 and t == 0),
-                stop=(s == PASSES - 1 and t == PACK - 1),
+                out=acc,
+                lhsT=stationary[0].bitcast(FP8X4),
+                lhsT_scale=stationary[1],
+                rhs=moving[0].bitcast(FP8X4),
+                rhs_scale=moving[1],
+                start=start,
+                stop=stop,
             )
 
-        def first_layer_pass(name, matrix, e, s, banks):
-            weights = quantized(interleave_in_quarters(load(matrix[e], s), VECTOR_COLUMNS[name, e])[:], "weight")
-            for t in range(PACK):
-                for u in range(SLOT_TILES):
-                    multiply(banks[u], weights, t * P, e, u, s, t)
+        def columns_of(operand, first, count):
+            return [part[:, first:first + count] for part in operand]
 
-        def by_slot(acc):
-            return acc[:].rearrange("p (t c) -> p c t", t=PACK)
+        def slots_of(s, first, count):
+            return columns_of((slot_words[s], slot_scales[s // PLANES][4 * (s % PLANES):P]), first, count)
 
-        def sigmoids(e, banks):
-            sig = keep.tile([P, C, PACK], F32, name=f"sig{e}", align_bytes=64)
+        def slots_stationary_pass(name, matrix, s, banks):
+            weights = quantized(interleave(load(matrix[0], s), VECTOR_COLUMNS[name, 0])[:], "weight")
             for u in range(SLOT_TILES):
-                nc.scalar.activation(sig[:, u * P:(u + 1) * P], by_slot(banks[u]), SIGMOID)
-            return sig
+                product(banks[u][:], slots_of(s, u * P, P), columns_of(weights, 0, H), s == 0, s == PASSES - 1)
 
-        def pieces(e):
-            return [slice(sum(PIECES[e][:r]), sum(PIECES[e][:r + 1])) for r in range(len(PIECES[e]))]
+        def by_pair(acc):
+            return acc[:].rearrange("s (p w r) -> s w p r", w=2, r=2)
 
-        def hidden_values(e, piece, banks, sig):
-            count = piece.stop - piece.start
-            hidden = keep.tile([P, count * PACK], BF16, name=f"hidden{e}_{piece.start}", align_bytes=64)
-            inside = slice(piece.start % P, piece.start % P + count)
-            nc.vector.tensor_tensor(hidden[:].rearrange("p (c t) -> p c t", t=PACK), by_slot(banks[piece.start // P])[:, inside], sig[:, piece], MULT)
+        def turned_hidden_values(u, acc, sig):
+            hidden = keep.tile([P, 2, P, 2], BF16, name=f"hidden{u}")
+            nc.vector.tensor_tensor(hidden[:], by_pair(acc), sig[:, u], MULT)
+            pairs = hidden[:].rearrange("s w p r -> s (w p r)").bitcast(F32)
+            turned = bank(TURN_BANK + u, f"turned{u}")
+            for w in range(2):
+                nc.tensor.transpose(turned[:, w * P:(w + 1) * P], pairs[:, w * P:(w + 1) * P], identity[:])
+            woven = values_tile(P)
+            nc.scalar.copy(woven[:].bitcast(F32).rearrange("p (c w) -> p c w", w=2), turned[:, :2 * P].rearrange("p (w c) -> p c w", w=2))
+            return woven
+
+        def quarter(banks, weights, first, s, t, u, count, start, stop):
+            in_bank = 512 // count
+            acc = banks[u + t // in_bank][:, t % in_bank * count:(t % in_bank + 1) * count]
+            product(acc, columns_of(weights, first, P), slots_of(s, C + u * P, count), start, stop)
+
+        def weights_stationary_pass(name, matrix, s, banks, count):
+            weights = quantized(interleave_in_quarters(load(matrix[1], s), VECTOR_COLUMNS[name, 1])[:], "weight")
+            in_bank = 512 // count
+            for t in range(PACK):
+                for u in range(C // count):
+                    quarter(banks, weights, t * P, s, t, u, count, s == 0 and t % in_bank == 0, s == PASSES - 1 and t % in_bank == in_bank - 1)
+
+        def hidden_values(hidden, piece, banks, sig):
+            inside = slice(piece.start % P, piece.start % P + piece.stop - piece.start)
+            nc.vector.tensor_tensor(
+                hidden.rearrange("p (c w r) -> p c w r", w=2, r=2),
+                banks[piece.start // P][:].rearrange("p (w r c) -> p c w r", w=2, r=2)[:, inside],
+                sig[:].rearrange("p w c r -> p c w r")[:, piece],
+                MULT,
+            )
             return hidden
 
-        def second_layer(e, r, second, moving):
-            h_codes, h_scales = moving
-            count = PIECES[e][r]
-            y = bank(Y_BANK + r, f"y{e}{r}")
-            for q, (codes, scales) in enumerate(second):
-                nc.tensor.matmul_mx(
-                    out=y[:, q * count:(q + 1) * count],
-                    lhsT=codes.bitcast(FP8X4),
-                    lhsT_scale=scales,
-                    rhs=h_codes[:].bitcast(FP8X4),
-                    rhs_scale=h_scales[:],
-                    start=True,
-                    stop=True,
-                )
-            result = keep.tile([P, ROW_TILES * count], F32, name=f"result{e}{r}")
-            nc.scalar.copy(result[:], y[:, :ROW_TILES * count])
-            return result
+        def second_layer(results, second, moving, banks):
+            count = results[0].shape[2]
+            sums = [bank(b, "y") for b in banks]
+            for q in range(ROW_TILES):
+                product(sums[q % len(sums)][:, q * count:(q + 1) * count], second[q], columns_of(moving, 0, count), True, True)
+            share = ROW_TILES // len(sums)
+            for g, y in enumerate(sums):
+                nc.scalar.copy(results[g], y[:, :ROW_TILES * count].rearrange("p (q c) -> p q c", q=ROW_TILES)[:, g * share:(g + 1) * share])
 
         def scatter(e, piece, result, gate_sb):
-            count = piece.stop - piece.start
-            first = e * C + piece.start
+            first, end = e * C + piece.start, e * C + piece.stop
             for q in range(ROW_TILES):
-                nc.vector.tensor_tensor(
-                    placed[q][:].indirect(dst_sb[:, first // LIST:(first + count) // LIST]),
-                    result[:, q * count:(q + 1) * count],
-                    gate_sb[:, first:first + count],
-                    MULT,
-                )
+                nc.vector.tensor_tensor(placed[q][:].indirect(dst_sb[:, first // LIST:end // LIST]), result[:, q, piece], gate_sb[:, first:end], MULT)
 
         def spread_gate():
             share = E * C // P
             row = keep.tile([P, E * C], F32, name="gate_row")
             nc.vector.memset(row[:P - 1, :], 0.0)
             nc.scalar.dma_start(row[P - 1:, :], gate[0:1, :])
-            upright = bank(Y_BANK + 1, "upright")
+            upright = bank(TURN_BANK + 1, "upright")
             for c in range(share):
                 nc.tensor.transpose(upright[:, c * P:(c + 1) * P], row[:, c * P:(c + 1) * P], identity[:])
             column = keep.tile([P, share], F32, name="gate_column")
             nc.scalar.copy(column[:], upright[:, P - 1::P])
-            spread = bank(Y_BANK, "spread")
+            spread = bank(TURN_BANK, "spread")
             for c in range(share):
                 nc.tensor.transpose(spread[:, c * P:(c + 1) * P], column[:, c:c + 1].to_broadcast([P, P]), identity[:])
             gate_sb = keep.tile([P, E * C], F32, name="gate_sb")
@@ -201,28 +206,36 @@ def tile_moe_two_glu_sigmoid_kernel(tc, xT, w1, w3, w2, gate, offs, dst, out):
 
         a_banks = banks_of(A_BANK, "a")
         for s in range(PASSES):
-            first_layer_pass("w1", w1, 0, s, a_banks)
-        sig = sigmoids(0, a_banks)
+            slots_stationary_pass("w1", w1, s, a_banks)
+        sig = keep.tile([P, SLOT_TILES, 2, P, 2], F32, name="sig0", align_bytes=64)
+        for u in range(SLOT_TILES):
+            nc.scalar.activation(sig[:, u], by_pair(a_banks[u]), SIGMOID)
         b_banks = banks_of(B_BANK, "b")
         for s in range(PASSES):
-            first_layer_pass("w3", w3, 0, s, b_banks)
-        codes, scales = quantized(interleave(load(w2[0], 0), VECTOR_COLUMNS["w2", 0])[:], "second")
-        second = [(codes[:, q * P:(q + 1) * P], scales[:, q * P:(q + 1) * P]) for q in range(ROW_TILES)]
+            slots_stationary_pass("w3", w3, s, b_banks)
+        weights = quantized(interleave(load(w2[0], 0), VECTOR_COLUMNS["w2", 0])[:], "second")
+        second = [columns_of(weights, q * P, P) for q in range(ROW_TILES)]
         nc.sync.dma_start(dst_sb[:], dst)
 
         a_banks = banks_of(A_BANK, "a")
+        result = keep.tile([P, ROW_TILES, C], F32, name="result0")
+        tiles = [slice(u * P, (u + 1) * P) for u in range(SLOT_TILES)]
         for s in range(PASSES):
-            first_layer_pass("w1", w1, 1, s, a_banks)
+            weights_stationary_pass("w1", w1, s, a_banks, C)
             if s == 0:
-                hidden = [hidden_values(0, piece, b_banks, sig) for piece in pieces(0)]
-                results = [second_layer(0, r, second, quantized(values[:], "hidden")) for r, values in enumerate(hidden)]
-            if s in (1, 2):
-                scatter(0, pieces(0)[s - 1], results[s - 1], gate_sb)
-        b_banks = banks_of(B_BANK, "b")
-        for s in range(PASSES - 1):
-            first_layer_pass("w3", w3, 1, s, b_banks)
+                woven = [turned_hidden_values(u, b_banks[u], sig) for u in range(SLOT_TILES)]
             if s == 1:
-                sig = sigmoids(1, a_banks)
+                for u in range(SLOT_TILES):
+                    second_layer([result[:, :, tiles[u]]], second, quantized(woven[u][:], "hidden"), [Y_BANK + u])
+            if s in (2, 3):
+                scatter(0, tiles[s - 2], result, gate_sb)
+        b_banks = banks_of(B_BANK, "b")
+        sig = keep.tile([P, 2, C, 2], F32, name="sig1", align_bytes=64)
+        for s in range(PASSES - 1):
+            weights_stationary_pass("w3", w3, s, b_banks, P)
+            if s == 1:
+                for w in range(2):
+                    nc.scalar.activation(sig[:, w], a_banks[w][:].rearrange("p (r c) -> p c r", r=2), SIGMOID)
 
         halves = [values_tile(H // 2) for side in range(2)]
         for v in range(2):
@@ -231,21 +244,25 @@ def tile_moe_two_glu_sigmoid_kernel(tc, xT, w1, w3, w2, gate, offs, dst, out):
             for side, copy in enumerate((nc.vector.tensor_copy, nc.scalar.copy)):
                 copy(halves[side][:].rearrange("p (t m j) -> p m j t", t=2, j=PACK)[:, :, rows], source[:, :, :, 2 * side:2 * side + 2])
         weights = [quantized(values[:], "last") for values in halves]
-        for side in range(2):
-            for u in range(SLOT_TILES):
-                for t in range(2):
-                    multiply(b_banks[u], weights[side], t * P, 1, u, PASSES - 1, 2 * side + t)
+        for u in range(SLOT_TILES):
+            order = [(t + 2 * u) % PACK for t in range(PACK)]
+            for t in order:
+                quarter(b_banks, weights[t // 2], t % 2 * P, PASSES - 1, t, u, P, False, t == order[-1])
 
         raw = load(w2[1], 0)
         columns = [values_tile(P) for q in range(ROW_TILES)]
         for q, copy in enumerate((nc.vector.tensor_copy, nc.scalar.copy)):
             weave(copy, columns[q][:], raw[:, :, q * P:(q + 1) * P])
-        hidden = [hidden_values(1, pieces(1)[0], b_banks, sig)]
-        second = [[part[:] for part in quantized(values[:], "second_half")] for values in columns]
-        results = [second_layer(1, 0, second, quantized(hidden[0][:], "hidden"))]
-        hidden.extend(hidden_values(1, piece, b_banks, sig) for piece in pieces(1)[1:])
-        results.extend(second_layer(1, r, second, quantized(hidden[r][:], "hidden")) for r in range(1, len(hidden)))
-        for piece, result in zip(pieces(1), results):
+        first, middle, last = PIECES
+        result = keep.tile([P, ROW_TILES, C], F32, name="result1")
+        hidden = [hidden_values(raw[:, 0, :P].bitcast(BF16), first, b_banks, sig)]
+        second = [columns_of(quantized(values[:], "second_half"), 0, P) for values in columns]
+        second_layer([result[:, q:q + 1, first] for q in range(ROW_TILES)], second, quantized(hidden[0], "hidden"), [A_BANK, A_BANK + 1])
+        hidden.append(hidden_values(columns[0][:, :(middle.stop - middle.start) * PACK], middle, b_banks, sig))
+        hidden.append(hidden_values(columns[1][:], last, b_banks, sig))
+        for r in (1, 2):
+            second_layer([result[:, :, PIECES[r]]], second, quantized(hidden[r], "hidden"), [Y_BANK + r - 1])
+        for piece in PIECES:
             scatter(1, piece, result, gate_sb)
         for q in range(ROW_TILES):
             nc.sync.dma_start(out[q * P:(q + 1) * P, :], placed[q][:])

@@ -9,6 +9,7 @@ PACK = 4
 K_PASS = P * PACK
 PASSES = K // K_PASS
 PLANES = 4
+BLOCK = 32
 LIST = 16
 SLOT_TILES = C // P
 ROW_TILES = N // P
@@ -125,38 +126,29 @@ def tile_moe_two_glu_sigmoid_kernel(tc, xT, w1, w3, w2, gate, offs, dst, out):
         def by_pair(acc):
             return acc[:].rearrange("s (p w r) -> s w p r", w=2, r=2)
 
-        def turned_hidden_values(u, acc, sig):
+        def turned_hidden_values(woven, u, acc, sig):
             hidden = keep.tile([P, 2, P, 2], BF16, name=f"hidden{u}")
             nc.vector.tensor_tensor(hidden[:], by_pair(acc), sig[:, u], MULT)
             pairs = hidden[:].rearrange("s w p r -> s (w p r)").bitcast(F32)
             turned = bank(TURN_BANK + u, f"turned{u}")
             for w in range(2):
                 nc.tensor.transpose(turned[:, w * P:(w + 1) * P], pairs[:, w * P:(w + 1) * P], identity[:])
-            woven = values_tile(P)
-            nc.scalar.copy(woven[:].bitcast(F32).rearrange("p (c w) -> p c w", w=2), turned[:, :2 * P].rearrange("p (w c) -> p c w", w=2))
-            return woven
+            nc.scalar.copy(woven[:].bitcast(F32).rearrange("p (c w) -> p c w", w=2)[:, u * P:(u + 1) * P], turned[:, :2 * P].rearrange("p (w c) -> p c w", w=2))
 
-        def quarter(banks, weights, first, s, t, u, count, start, stop):
-            in_bank = 512 // count
-            acc = banks[u + t // in_bank][:, t % in_bank * count:(t % in_bank + 1) * count]
-            product(acc, columns_of(weights, first, P), slots_of(s, C + u * P, count), start, stop)
+        def quarter(banks, weights, first, s, t):
+            w, r = divmod(t, 2)
+            product(banks[w][:, r * C:(r + 1) * C], columns_of(weights, first, P), slots_of(s, C, C), s == 0 and r == 0, s == PASSES - 1 and r == 1)
 
-        def weights_stationary_pass(name, matrix, s, banks, count):
+        def weights_stationary_pass(name, matrix, s, banks):
             weights = quantized(interleave_in_quarters(load(matrix[1], s), VECTOR_COLUMNS[name, 1])[:], "weight")
-            in_bank = 512 // count
             for t in range(PACK):
-                for u in range(C // count):
-                    quarter(banks, weights, t * P, s, t, u, count, s == 0 and t % in_bank == 0, s == PASSES - 1 and t % in_bank == in_bank - 1)
+                quarter(banks, weights, t * P, s, t)
 
-        def hidden_values(hidden, piece, banks, sig):
-            inside = slice(piece.start % P, piece.start % P + piece.stop - piece.start)
-            nc.vector.tensor_tensor(
-                hidden.rearrange("p (c w r) -> p c w r", w=2, r=2),
-                banks[piece.start // P][:].rearrange("p (w r c) -> p c w r", w=2, r=2)[:, inside],
-                sig[:].rearrange("p w c r -> p c w r")[:, piece],
-                MULT,
-            )
-            return hidden
+        def by_slot(acc):
+            return acc[:].rearrange("p (r c) -> p c r", r=2)
+
+        def hidden_pair(hidden, piece, w, banks, sig):
+            nc.vector.tensor_tensor(hidden.rearrange("p (c w r) -> p c w r", w=2, r=2)[:, piece, w], by_slot(banks[w])[:, piece], sig[:, w, piece], MULT)
 
         def second_layer(results, second, moving, banks):
             count = results[0].shape[2]
@@ -173,20 +165,15 @@ def tile_moe_two_glu_sigmoid_kernel(tc, xT, w1, w3, w2, gate, offs, dst, out):
                 nc.vector.tensor_tensor(placed[q][:].indirect(dst_sb[:, first // LIST:end // LIST]), result[:, q, piece], gate_sb[:, first:end], MULT)
 
         def spread_gate():
-            share = E * C // P
-            row = keep.tile([P, E * C], F32, name="gate_row")
-            nc.vector.memset(row[:P - 1, :], 0.0)
-            nc.scalar.dma_start(row[P - 1:, :], gate[0:1, :])
-            upright = bank(TURN_BANK + 1, "upright")
-            for c in range(share):
-                nc.tensor.transpose(upright[:, c * P:(c + 1) * P], row[:, c * P:(c + 1) * P], identity[:])
-            column = keep.tile([P, share], F32, name="gate_column")
-            nc.scalar.copy(column[:], upright[:, P - 1::P])
-            spread = bank(TURN_BANK, "spread")
-            for c in range(share):
-                nc.tensor.transpose(spread[:, c * P:(c + 1) * P], column[:, c:c + 1].to_broadcast([P, P]), identity[:])
-            gate_sb = keep.tile([P, E * C], F32, name="gate_sb")
-            nc.scalar.copy(gate_sb[:], spread[:])
+            runs = E * C // BLOCK
+            cut = keep.tile([P, BLOCK], F32, name="gate_cut", align_bytes=256)
+            nc.scalar.dma_start(cut[:], gate[:P // runs, :].rearrange("r (g b) -> (r g) b", b=BLOCK))
+            upright = keep.tile([P, BLOCK], F32, name="gate_upright", align_bytes=64)
+            nc.vector.transpose(upright[:], cut[:])
+            repeated = keep.tile([P, runs, BLOCK], F32, name="gate_repeated", align_bytes=64)
+            nc.vector.tensor_copy(repeated[:], upright[:, :runs].unsqueeze(2).to_broadcast([P, runs, BLOCK]))
+            gate_sb = keep.tile([P, E * C], F32, name="gate_sb", align_bytes=64)
+            nc.vector.transpose(gate_sb[:], repeated[:].rearrange("p g b -> p (g b)"))
             return gate_sb
 
         def banks_of(first_bank, name):
@@ -221,21 +208,22 @@ def tile_moe_two_glu_sigmoid_kernel(tc, xT, w1, w3, w2, gate, offs, dst, out):
         result = keep.tile([P, ROW_TILES, C], F32, name="result0")
         tiles = [slice(u * P, (u + 1) * P) for u in range(SLOT_TILES)]
         for s in range(PASSES):
-            weights_stationary_pass("w1", w1, s, a_banks, C)
+            weights_stationary_pass("w1", w1, s, a_banks)
             if s == 0:
-                woven = [turned_hidden_values(u, b_banks[u], sig) for u in range(SLOT_TILES)]
-            if s == 1:
+                woven = values_tile(C)
                 for u in range(SLOT_TILES):
-                    second_layer([result[:, :, tiles[u]]], second, quantized(woven[u][:], "hidden"), [Y_BANK + u])
+                    turned_hidden_values(woven, u, b_banks[u], sig)
+            if s == 1:
+                second_layer([result[:]], second, quantized(woven[:], "hidden"), [Y_BANK])
             if s in (2, 3):
                 scatter(0, tiles[s - 2], result, gate_sb)
         b_banks = banks_of(B_BANK, "b")
         sig = keep.tile([P, 2, C, 2], F32, name="sig1", align_bytes=64)
         for s in range(PASSES - 1):
-            weights_stationary_pass("w3", w3, s, b_banks, P)
+            weights_stationary_pass("w3", w3, s, b_banks)
             if s == 1:
                 for w in range(2):
-                    nc.scalar.activation(sig[:, w], a_banks[w][:].rearrange("p (r c) -> p c r", r=2), SIGMOID)
+                    nc.scalar.activation(sig[:, w], by_slot(a_banks[w]), SIGMOID)
 
         halves = [values_tile(H // 2) for side in range(2)]
         for v in range(2):
@@ -244,24 +232,30 @@ def tile_moe_two_glu_sigmoid_kernel(tc, xT, w1, w3, w2, gate, offs, dst, out):
             for side, copy in enumerate((nc.vector.tensor_copy, nc.scalar.copy)):
                 copy(halves[side][:].rearrange("p (t m j) -> p m j t", t=2, j=PACK)[:, :, rows], source[:, :, :, 2 * side:2 * side + 2])
         weights = [quantized(values[:], "last") for values in halves]
-        for u in range(SLOT_TILES):
-            order = [(t + 2 * u) % PACK for t in range(PACK)]
-            for t in order:
-                quarter(b_banks, weights[t // 2], t % 2 * P, PASSES - 1, t, u, P, False, t == order[-1])
+        for t in range(PACK):
+            quarter(b_banks, weights[t // 2], t % 2 * P, PASSES - 1, t)
 
         raw = load(w2[1], 0)
         columns = [values_tile(P) for q in range(ROW_TILES)]
-        for q, copy in enumerate((nc.vector.tensor_copy, nc.scalar.copy)):
-            weave(copy, columns[q][:], raw[:, :, q * P:(q + 1) * P])
+        for q in range(ROW_TILES):
+            weave(nc.scalar.copy, columns[q][:], raw[:, :, q * P:(q + 1) * P])
         first, middle, last = PIECES
         result = keep.tile([P, ROW_TILES, C], F32, name="result1")
-        hidden = [hidden_values(raw[:, 0, :P].bitcast(BF16), first, b_banks, sig)]
-        second = [columns_of(quantized(values[:], "second_half"), 0, P) for values in columns]
-        second_layer([result[:, q:q + 1, first] for q in range(ROW_TILES)], second, quantized(hidden[0], "hidden"), [A_BANK, A_BANK + 1])
-        hidden.append(hidden_values(columns[0][:, :(middle.stop - middle.start) * PACK], middle, b_banks, sig))
-        hidden.append(hidden_values(columns[1][:], last, b_banks, sig))
-        for r in (1, 2):
-            second_layer([result[:, :, PIECES[r]]], second, quantized(hidden[r], "hidden"), [Y_BANK + r - 1])
+        hidden = values_tile(C)[:]
+
+        def moving(piece):
+            return quantized(hidden[:, piece.start * PACK:piece.stop * PACK], "hidden")
+
+        hidden_pair(hidden, slice(0, C), 0, b_banks, sig)
+        second = [columns_of(quantized(columns[0][:], "second_half"), 0, P)]
+        hidden_pair(hidden, first, 1, b_banks, sig)
+        hidden_pair(hidden, middle, 1, b_banks, sig)
+        early = moving(first)
+        second.append(columns_of(quantized(columns[1][:], "second_half"), 0, P))
+        second_layer([result[:, q:q + 1, first] for q in range(ROW_TILES)], second, early, [A_BANK, A_BANK + 1])
+        hidden_pair(hidden, last, 1, b_banks, sig)
+        second_layer([result[:, :, middle]], second, moving(middle), [Y_BANK])
+        second_layer([result[:, :, last]], second, moving(last), [Y_BANK + 1])
         for piece in PIECES:
             scatter(1, piece, result, gate_sb)
         for q in range(ROW_TILES):

@@ -26,11 +26,16 @@ MULT = mybir.AluOpType.mult
 
 RUN = 2
 
-VECTOR_COLUMNS = {("x", 0): 64, ("w1", 0): 192, ("w3", 0): 256, ("w2", 0): 64, ("w1", 1): 192, ("w3", 1): 256}
+VECTOR_COLUMNS = {("x", 0): 64, ("w1", 0): 192, ("w3", 0): 256, ("w2", 0): 64}
+W1_SHARES = (240, 176, 176, 176, 176)
+W3_SHARES = (224, 256, 288, 304)
 
 PIECES = (slice(0, 64), slice(64, 128), slice(128, 256))
 
-A_BANK, B_BANK, Y_BANK, TURN_BANK = 0, 2, 4, 6
+ALL = slice(0, H)
+LEFT, RIGHT = slice(0, H // 2), slice(H // 2, H)
+
+A_BANK, B_BANK, Y_BANK, TURN_BANK = 0, 2, 5, 6
 
 
 def tile_moe_two_glu_sigmoid_kernel(tc, xT, w1, w3, w2, gate, offs, dst, out):
@@ -64,22 +69,14 @@ def tile_moe_two_glu_sigmoid_kernel(tc, xT, w1, w3, w2, gate, offs, dst, out):
         def values_tile(width):
             return work.tile([P, width * PACK], BF16, name=f"grouped{width}", align_bytes=64)
 
-        def weave(copy, grouped, raw):
-            copy(grouped.rearrange("p (c i j) -> p c j i", i=RUN, j=PACK), raw.rearrange("p j (c i) -> p c j i", i=RUN))
+        def weave(copy, grouped, raw, rows=slice(0, PACK)):
+            copy(grouped.rearrange("p (c i j) -> p c j i", i=RUN, j=PACK)[:, :, rows], raw.rearrange("p j (c i) -> p c j i", i=RUN))
 
         def interleave(raw, cut):
             width = raw.shape[2]
             grouped = values_tile(width)
             weave(nc.vector.tensor_copy, grouped[:, :cut * PACK], raw[:, :, :cut])
             weave(nc.scalar.copy, grouped[:, cut * PACK:], raw[:, :, cut:])
-            return grouped
-
-        def interleave_in_quarters(raw, cut):
-            grouped = values_tile(H)
-            to = grouped[:].rearrange("p (t m j) -> p m j t", t=PACK, j=PACK)
-            source = raw[:].rearrange("p j (m t) -> p m j t", t=PACK)
-            nc.vector.tensor_copy(to[:, :cut // PACK], source[:, :cut // PACK])
-            nc.scalar.copy(to[:, cut // PACK:], source[:, cut // PACK:])
             return grouped
 
         def quantize(values, codes, scales):
@@ -118,37 +115,37 @@ def tile_moe_two_glu_sigmoid_kernel(tc, xT, w1, w3, w2, gate, offs, dst, out):
         def slots_of(s, first, count):
             return columns_of((slot_words[s], slot_scales[s // PLANES][4 * (s % PLANES):P]), first, count)
 
-        def slots_stationary_pass(name, matrix, s, banks):
-            weights = quantized(interleave(load(matrix[0], s), VECTOR_COLUMNS[name, 0])[:], "weight")
-            for u in range(SLOT_TILES):
-                product(banks[u][:], slots_of(s, u * P, P), columns_of(weights, 0, H), s == 0, s == PASSES - 1)
+        def first_layer_pass(raw, cut, e, s, groups):
+            multiply(quantized(interleave(raw, cut)[:], "weight"), 0, e, s, groups)
 
-        def by_pair(acc):
-            return acc[:].rearrange("s (p w r) -> s w p r", w=2, r=2)
+        def multiply(weights, first, e, s, groups):
+            for u, columns, acc in groups:
+                count = columns.stop - columns.start
+                product(acc[:, :count], slots_of(s, e * C + u * P, P), columns_of(weights, columns.start - first, count), s == 0, s == PASSES - 1)
 
-        def turned_hidden_values(woven, u, acc, sig):
-            hidden = keep.tile([P, 2, P, 2], BF16, name=f"hidden{u}")
-            nc.vector.tensor_tensor(hidden[:], by_pair(acc), sig[:, u], MULT)
+        def by_pair(columns):
+            return columns.rearrange("s (p w r) -> s w p r", w=2, r=2)
+
+        def sigmoids(sig, groups):
+            for u, columns, acc in groups:
+                nc.scalar.activation(sig[:, u], by_pair(acc[:]), SIGMOID)
+
+        def hidden_pairs(groups, sig):
+            hidden = [keep.tile([P, 2, P, 2], BF16, name=f"hidden{u}") for u in range(SLOT_TILES)]
+            for u, columns, acc in groups:
+                words = slice(columns.start // PACK, columns.stop // PACK)
+                nc.vector.tensor_tensor(hidden[u][:, :, words], by_pair(acc[:, :columns.stop - columns.start]), sig[:, u, :, words], MULT)
+            return hidden
+
+        def turn(u, hidden):
             pairs = hidden[:].rearrange("s w p r -> s (w p r)").bitcast(F32)
             turned = bank(TURN_BANK + u, f"turned{u}")
             for w in range(2):
                 nc.tensor.transpose(turned[:, w * P:(w + 1) * P], pairs[:, w * P:(w + 1) * P], identity[:])
-            nc.scalar.copy(woven[:].bitcast(F32).rearrange("p (c w) -> p c w", w=2)[:, u * P:(u + 1) * P], turned[:, :2 * P].rearrange("p (w c) -> p c w", w=2))
+            return turned[:, :2 * P].rearrange("p (w c) -> p c w", w=2)
 
-        def quarter(banks, weights, first, s, t):
-            w, r = divmod(t, 2)
-            product(banks[w][:, r * C:(r + 1) * C], columns_of(weights, first, P), slots_of(s, C, C), s == 0 and r == 0, s == PASSES - 1 and r == 1)
-
-        def weights_stationary_pass(name, matrix, s, banks):
-            weights = quantized(interleave_in_quarters(load(matrix[1], s), VECTOR_COLUMNS[name, 1])[:], "weight")
-            for t in range(PACK):
-                quarter(banks, weights, t * P, s, t)
-
-        def by_slot(acc):
-            return acc[:].rearrange("p (r c) -> p c r", r=2)
-
-        def hidden_pair(hidden, piece, w, banks, sig):
-            nc.vector.tensor_tensor(hidden.rearrange("p (c w r) -> p c w r", w=2, r=2)[:, piece, w], by_slot(banks[w])[:, piece], sig[:, w, piece], MULT)
+        def lay(woven, turned):
+            nc.scalar.copy(woven.bitcast(F32).rearrange("p (c w) -> p c w", w=2), turned)
 
         def second_layer(results, second, moving, banks):
             count = results[0].shape[2]
@@ -159,10 +156,9 @@ def tile_moe_two_glu_sigmoid_kernel(tc, xT, w1, w3, w2, gate, offs, dst, out):
             for g, y in enumerate(sums):
                 nc.scalar.copy(results[g], y[:, :ROW_TILES * count].rearrange("p (q c) -> p q c", q=ROW_TILES)[:, g * share:(g + 1) * share])
 
-        def scatter(e, piece, result, gate_sb):
+        def scatter(e, piece, q, values, gate_sb):
             first, end = e * C + piece.start, e * C + piece.stop
-            for q in range(ROW_TILES):
-                nc.vector.tensor_tensor(placed[q][:].indirect(dst_sb[:, first // LIST:end // LIST]), result[:, q, piece], gate_sb[:, first:end], MULT)
+            nc.vector.tensor_tensor(placed[q][:].indirect(dst_sb[:, first // LIST:end // LIST]), values, gate_sb[:, first:end], MULT)
 
         def spread_gate():
             runs = E * C // BLOCK
@@ -176,8 +172,8 @@ def tile_moe_two_glu_sigmoid_kernel(tc, xT, w1, w3, w2, gate, offs, dst, out):
             nc.vector.transpose(gate_sb[:], repeated[:].rearrange("p g b -> p (g b)"))
             return gate_sb
 
-        def banks_of(first_bank, name):
-            return [bank(first_bank + u, f"{name}{u}") for u in range(SLOT_TILES)]
+        def whole_groups(first_bank, name):
+            return [(u, ALL, bank(first_bank + u, f"{name}{u}")) for u in range(SLOT_TILES)]
 
         for s in range(PASSES):
             raw = load(xT, s)
@@ -191,72 +187,75 @@ def tile_moe_two_glu_sigmoid_kernel(tc, xT, w1, w3, w2, gate, offs, dst, out):
                 if s % PLANES == PLANES - 1 or s == PASSES - 1:
                     gather(slot_scales[s // PLANES], token_scales[s // PLANES], e)
 
-        a_banks = banks_of(A_BANK, "a")
+        a_groups = whole_groups(A_BANK, "a")
         for s in range(PASSES):
-            slots_stationary_pass("w1", w1, s, a_banks)
+            first_layer_pass(load(w1[0], s), VECTOR_COLUMNS["w1", 0], 0, s, a_groups)
         sig = keep.tile([P, SLOT_TILES, 2, P, 2], F32, name="sig0", align_bytes=64)
-        for u in range(SLOT_TILES):
-            nc.scalar.activation(sig[:, u], by_pair(a_banks[u]), SIGMOID)
-        b_banks = banks_of(B_BANK, "b")
+        sigmoids(sig, a_groups)
+        b_groups = whole_groups(B_BANK, "b")
         for s in range(PASSES):
-            slots_stationary_pass("w3", w3, s, b_banks)
+            first_layer_pass(load(w3[0], s), VECTOR_COLUMNS["w3", 0], 0, s, b_groups)
         weights = quantized(interleave(load(w2[0], 0), VECTOR_COLUMNS["w2", 0])[:], "second")
         second = [columns_of(weights, q * P, P) for q in range(ROW_TILES)]
         nc.sync.dma_start(dst_sb[:], dst)
+        hidden = hidden_pairs(b_groups, sig)
 
-        a_banks = banks_of(A_BANK, "a")
-        result = keep.tile([P, ROW_TILES, C], F32, name="result0")
-        tiles = [slice(u * P, (u + 1) * P) for u in range(SLOT_TILES)]
+        a_groups = whole_groups(A_BANK, "a")
+        y = bank(Y_BANK, "y")
         for s in range(PASSES):
-            weights_stationary_pass("w1", w1, s, a_banks)
+            raw = load(w1[1], s)
+            first_layer_pass(raw, W1_SHARES[s], 1, s, a_groups)
             if s == 0:
-                woven = values_tile(C)
+                woven = raw[:, 0].bitcast(BF16)
                 for u in range(SLOT_TILES):
-                    turned_hidden_values(woven, u, b_banks[u], sig)
-            if s == 1:
-                second_layer([result[:]], second, quantized(woven[:], "hidden"), [Y_BANK])
-            if s in (2, 3):
-                scatter(0, tiles[s - 2], result, gate_sb)
-        b_banks = banks_of(B_BANK, "b")
-        sig = keep.tile([P, 2, C, 2], F32, name="sig1", align_bytes=64)
+                    lay(woven[:, u * P * PACK:(u + 1) * P * PACK], turn(u, hidden[u]))
+                moving = quantized(woven, "hidden")
+                for q in range(ROW_TILES):
+                    product(y[:, q * C:(q + 1) * C], second[q], columns_of(moving, 0, C), True, True)
+            else:
+                u, q = divmod(s - 1, ROW_TILES)
+                nc.scalar.copy(raw[:, 0, :P], y[:, q * C + u * P:q * C + (u + 1) * P])
+                scatter(0, slice(u * P, (u + 1) * P), q, raw[:, 0, :P], gate_sb)
+
+        b_groups = [(u, columns, bank(B_BANK + g, f"b{g}")) for g, (u, columns) in enumerate(((0, LEFT), (0, RIGHT), (1, ALL)))]
         for s in range(PASSES - 1):
-            weights_stationary_pass("w3", w3, s, b_banks)
+            raw = load(w3[1], s)
+            first_layer_pass(raw, W3_SHARES[s], 1, s, b_groups)
             if s == 1:
-                for w in range(2):
-                    nc.scalar.activation(sig[:, w], by_slot(a_banks[w]), SIGMOID)
+                sig = raw[:, :SLOT_TILES].rearrange("s u (w p r) -> s u w p r", w=2, r=2)
+                sigmoids(sig, a_groups)
 
-        halves = [values_tile(H // 2) for side in range(2)]
-        for v in range(2):
+        left, right = [values_tile(H // 2) for side in range(2)]
+        for v, (to_left, to_right) in enumerate(((nc.scalar.copy, nc.vector.tensor_copy), (nc.vector.tensor_copy, nc.scalar.copy))):
             rows = slice(2 * v, 2 * v + 2)
-            source = load(w3[1], PASSES - 1, rows)[:].rearrange("p j (m t) -> p m j t", t=PACK)
-            for side, copy in enumerate((nc.vector.tensor_copy, nc.scalar.copy)):
-                copy(halves[side][:].rearrange("p (t m j) -> p m j t", t=2, j=PACK)[:, :, rows], source[:, :, :, 2 * side:2 * side + 2])
-        weights = [quantized(values[:], "last") for values in halves]
-        for t in range(PACK):
-            quarter(b_banks, weights[t // 2], t % 2 * P, PASSES - 1, t)
+            piece = load(w3[1], PASSES - 1, rows)
+            weave(to_left, left[:], piece[:, :, LEFT], rows)
+            weave(to_right, right[:], piece[:, :, RIGHT], rows)
+        weights = packed(H, "weight")
+        for grouped, columns in ((left, LEFT), (right, RIGHT)):
+            quantize(grouped[:], weights[0][:, columns], weights[1][:, columns])
+        multiply(weights, 0, 1, PASSES - 1, b_groups)
 
-        raw = load(w2[1], 0)
-        columns = [values_tile(P) for q in range(ROW_TILES)]
-        for q in range(ROW_TILES):
-            weave(nc.scalar.copy, columns[q][:], raw[:, :, q * P:(q + 1) * P])
-        first, middle, last = PIECES
-        result = keep.tile([P, ROW_TILES, C], F32, name="result1")
-        hidden = values_tile(C)[:]
-
-        def moving(piece):
-            return quantized(hidden[:, piece.start * PACK:piece.stop * PACK], "hidden")
-
-        hidden_pair(hidden, slice(0, C), 0, b_banks, sig)
-        second = [columns_of(quantized(columns[0][:], "second_half"), 0, P)]
-        hidden_pair(hidden, first, 1, b_banks, sig)
-        hidden_pair(hidden, middle, 1, b_banks, sig)
-        early = moving(first)
-        second.append(columns_of(quantized(columns[1][:], "second_half"), 0, P))
-        second_layer([result[:, q:q + 1, first] for q in range(ROW_TILES)], second, early, [A_BANK, A_BANK + 1])
-        hidden_pair(hidden, last, 1, b_banks, sig)
-        second_layer([result[:, :, middle]], second, moving(middle), [Y_BANK])
-        second_layer([result[:, :, last]], second, moving(last), [Y_BANK + 1])
+        grouped = values_tile(N)
+        weave(nc.scalar.copy, grouped[:], load(w2[1], 0)[:])
+        hidden = hidden_pairs(b_groups, sig)
+        weights = quantized(grouped[:], "second")
+        second = [columns_of(weights, q * P, P) for q in range(ROW_TILES)]
+        turned = [turn(u, hidden[u]) for u in range(SLOT_TILES)]
+        result = keep.tile([P, ROW_TILES, C], F32, name="result")
+        first = PIECES[0]
+        results = [[result[:, q:q + 1, first] for q in range(ROW_TILES)]] + [[result[:, :, piece]] for piece in PIECES[1:]]
+        banks = [[A_BANK, A_BANK + 1], [Y_BANK], [B_BANK]]
+        moving = []
         for piece in PIECES:
-            scatter(1, piece, result, gate_sb)
+            count = piece.stop - piece.start
+            woven = values_tile(count)[:]
+            lay(woven, turned[piece.start // P][:, piece.start % P:piece.start % P + count])
+            moving.append(quantized(woven, "hidden"))
+        for r in range(len(PIECES)):
+            second_layer(results[r], second, moving[r], banks[r])
+        for piece in PIECES:
+            for q in range(ROW_TILES):
+                scatter(1, piece, q, result[:, q, piece], gate_sb)
         for q in range(ROW_TILES):
             nc.sync.dma_start(out[q * P:(q + 1) * P, :], placed[q][:])

@@ -33,9 +33,10 @@ W3_SHARES = (224, 256, 288, 304)
 PIECES = (slice(0, 64), slice(64, 128), slice(128, 256))
 
 ALL = slice(0, H)
-LEFT, RIGHT = slice(0, H // 2), slice(H // 2, H)
+QUARTERS = [slice(g * P, (g + 1) * P) for g in range(H // P)]
 
 A_BANK, B_BANK, Y_BANK, TURN_BANK = 0, 2, 5, 6
+LAST_B_BANKS = (2, 3, 4, 6, 7)
 
 
 def tile_moe_two_glu_sigmoid_kernel(tc, xT, w1, w3, w2, gate, offs, dst, out):
@@ -69,8 +70,8 @@ def tile_moe_two_glu_sigmoid_kernel(tc, xT, w1, w3, w2, gate, offs, dst, out):
         def values_tile(width):
             return work.tile([P, width * PACK], BF16, name=f"grouped{width}", align_bytes=64)
 
-        def weave(copy, grouped, raw, rows=slice(0, PACK)):
-            copy(grouped.rearrange("p (c i j) -> p c j i", i=RUN, j=PACK)[:, :, rows], raw.rearrange("p j (c i) -> p c j i", i=RUN))
+        def weave(copy, grouped, raw):
+            copy(grouped.rearrange("p (c i j) -> p c j i", i=RUN, j=PACK), raw.rearrange("p j (c i) -> p c j i", i=RUN))
 
         def interleave(raw, cut):
             width = raw.shape[2]
@@ -115,13 +116,19 @@ def tile_moe_two_glu_sigmoid_kernel(tc, xT, w1, w3, w2, gate, offs, dst, out):
         def slots_of(s, first, count):
             return columns_of((slot_words[s], slot_scales[s // PLANES][4 * (s % PLANES):P]), first, count)
 
-        def first_layer_pass(raw, cut, e, s, groups):
-            multiply(quantized(interleave(raw, cut)[:], "weight"), 0, e, s, groups)
-
-        def multiply(weights, first, e, s, groups):
+        def first_layer_pass(grouped, e, s, groups):
+            weights = quantized(grouped[:], "weight")
             for u, columns, acc in groups:
                 count = columns.stop - columns.start
-                product(acc[:, :count], slots_of(s, e * C + u * P, P), columns_of(weights, columns.start - first, count), s == 0, s == PASSES - 1)
+                product(acc[:, :count], slots_of(s, e * C + u * P, P), columns_of(weights, columns.start, count), s == 0, s == PASSES - 1)
+
+        def interleave_by_pair(raw, cut):
+            grouped = values_tile(H)
+            to = grouped[:].rearrange("k (w p r j) -> k p w j r", w=2, r=2, j=PACK)
+            source = raw[:].rearrange("k j (p w r) -> k p w j r", w=2, r=2)
+            nc.vector.tensor_copy(to[:, :cut // PACK], source[:, :cut // PACK])
+            nc.scalar.copy(to[:, cut // PACK:], source[:, cut // PACK:])
+            return grouped
 
         def by_pair(columns):
             return columns.rearrange("s (p w r) -> s w p r", w=2, r=2)
@@ -133,13 +140,12 @@ def tile_moe_two_glu_sigmoid_kernel(tc, xT, w1, w3, w2, gate, offs, dst, out):
         def hidden_pairs(groups, sig):
             hidden = [keep.tile([P, 2, P, 2], BF16, name=f"hidden{u}") for u in range(SLOT_TILES)]
             for u, columns, acc in groups:
-                words = slice(columns.start // PACK, columns.stop // PACK)
-                nc.vector.tensor_tensor(hidden[u][:, :, words], by_pair(acc[:, :columns.stop - columns.start]), sig[:, u, :, words], MULT)
+                nc.vector.tensor_tensor(hidden[u][:], by_pair(acc[:]), sig[:, u], MULT)
             return hidden
 
-        def turn(u, hidden):
+        def turn(b, hidden):
             pairs = hidden[:].rearrange("s w p r -> s (w p r)").bitcast(F32)
-            turned = bank(TURN_BANK + u, f"turned{u}")
+            turned = bank(b, "turned")
             for w in range(2):
                 nc.tensor.transpose(turned[:, w * P:(w + 1) * P], pairs[:, w * P:(w + 1) * P], identity[:])
             return turned[:, :2 * P].rearrange("p (w c) -> p c w", w=2)
@@ -189,12 +195,12 @@ def tile_moe_two_glu_sigmoid_kernel(tc, xT, w1, w3, w2, gate, offs, dst, out):
 
         a_groups = whole_groups(A_BANK, "a")
         for s in range(PASSES):
-            first_layer_pass(load(w1[0], s), VECTOR_COLUMNS["w1", 0], 0, s, a_groups)
+            first_layer_pass(interleave(load(w1[0], s), VECTOR_COLUMNS["w1", 0]), 0, s, a_groups)
         sig = keep.tile([P, SLOT_TILES, 2, P, 2], F32, name="sig0", align_bytes=64)
         sigmoids(sig, a_groups)
         b_groups = whole_groups(B_BANK, "b")
         for s in range(PASSES):
-            first_layer_pass(load(w3[0], s), VECTOR_COLUMNS["w3", 0], 0, s, b_groups)
+            first_layer_pass(interleave(load(w3[0], s), VECTOR_COLUMNS["w3", 0]), 0, s, b_groups)
         weights = quantized(interleave(load(w2[0], 0), VECTOR_COLUMNS["w2", 0])[:], "second")
         second = [columns_of(weights, q * P, P) for q in range(ROW_TILES)]
         nc.sync.dma_start(dst_sb[:], dst)
@@ -204,11 +210,11 @@ def tile_moe_two_glu_sigmoid_kernel(tc, xT, w1, w3, w2, gate, offs, dst, out):
         y = bank(Y_BANK, "y")
         for s in range(PASSES):
             raw = load(w1[1], s)
-            first_layer_pass(raw, W1_SHARES[s], 1, s, a_groups)
+            first_layer_pass(interleave(raw, W1_SHARES[s]), 1, s, a_groups)
             if s == 0:
                 woven = raw[:, 0].bitcast(BF16)
                 for u in range(SLOT_TILES):
-                    lay(woven[:, u * P * PACK:(u + 1) * P * PACK], turn(u, hidden[u]))
+                    lay(woven[:, u * P * PACK:(u + 1) * P * PACK], turn(TURN_BANK + u, hidden[u]))
                 moving = quantized(woven, "hidden")
                 for q in range(ROW_TILES):
                     product(y[:, q * C:(q + 1) * C], second[q], columns_of(moving, 0, C), True, True)
@@ -217,35 +223,42 @@ def tile_moe_two_glu_sigmoid_kernel(tc, xT, w1, w3, w2, gate, offs, dst, out):
                 nc.scalar.copy(raw[:, 0, :P], y[:, q * C + u * P:q * C + (u + 1) * P])
                 scatter(0, slice(u * P, (u + 1) * P), q, raw[:, 0, :P], gate_sb)
 
-        b_groups = [(u, columns, bank(B_BANK + g, f"b{g}")) for g, (u, columns) in enumerate(((0, LEFT), (0, RIGHT), (1, ALL)))]
+        b_groups = [(0, columns, bank(b, "b")) for columns, b in zip(QUARTERS, LAST_B_BANKS)] + [(1, ALL, bank(LAST_B_BANKS[-1], "b"))]
         for s in range(PASSES - 1):
             raw = load(w3[1], s)
-            first_layer_pass(raw, W3_SHARES[s], 1, s, b_groups)
+            first_layer_pass(interleave_by_pair(raw, W3_SHARES[s]), 1, s, b_groups)
             if s == 1:
-                sig = raw[:, :SLOT_TILES].rearrange("s u (w p r) -> s u w p r", w=2, r=2)
-                sigmoids(sig, a_groups)
+                sig = raw[:, :SLOT_TILES]
+                sigmoids(sig.rearrange("s u (w p r) -> s u w p r", w=2, r=2), a_groups)
 
-        left, right = [values_tile(H // 2) for side in range(2)]
-        for v, (to_left, to_right) in enumerate(((nc.scalar.copy, nc.vector.tensor_copy), (nc.vector.tensor_copy, nc.scalar.copy))):
+        quarters = [values_tile(P) for columns in QUARTERS]
+        for v in range(2):
             rows = slice(2 * v, 2 * v + 2)
-            piece = load(w3[1], PASSES - 1, rows)
-            weave(to_left, left[:], piece[:, :, LEFT], rows)
-            weave(to_right, right[:], piece[:, :, RIGHT], rows)
+            source = load(w3[1], PASSES - 1, rows)[:].rearrange("k j (half p w r) -> k w half p j r", half=2, w=2, r=2)
+            for g, grouped in enumerate(quarters):
+                w, half = divmod(g, 2)
+                copy = nc.vector.tensor_copy if w != v else nc.scalar.copy
+                copy(grouped[:].rearrange("k (p r j) -> k p j r", r=2, j=PACK)[:, :, rows], source[:, w, half])
         weights = packed(H, "weight")
-        for grouped, columns in ((left, LEFT), (right, RIGHT)):
-            quantize(grouped[:], weights[0][:, columns], weights[1][:, columns])
-        multiply(weights, 0, 1, PASSES - 1, b_groups)
+        for g, columns in enumerate(QUARTERS):
+            quantize(quarters[g][:], weights[0][:, columns], weights[1][:, columns])
+            product(b_groups[g][2][:, :P], slots_of(PASSES - 1, C, P), columns_of(weights, columns.start, P), False, True)
+            if g % 2:
+                pair = slice(columns.stop - 2 * P, columns.stop)
+                product(b_groups[-1][2][:, pair], slots_of(PASSES - 1, C + P, P), columns_of(weights, pair.start, 2 * P), False, columns.stop == H)
 
         grouped = values_tile(N)
         weave(nc.scalar.copy, grouped[:], load(w2[1], 0)[:])
-        hidden = hidden_pairs(b_groups, sig)
+        hidden = [keep.tile([P, 2, P, 2], BF16, name=f"hidden{u}") for u in range(SLOT_TILES)]
+        for u, columns, acc in b_groups:
+            nc.vector.tensor_tensor(hidden[u][:].rearrange("s w p r -> s (w p r)")[:, columns], acc[:, :columns.stop - columns.start], sig[:, u, columns], MULT)
         weights = quantized(grouped[:], "second")
         second = [columns_of(weights, q * P, P) for q in range(ROW_TILES)]
-        turned = [turn(u, hidden[u]) for u in range(SLOT_TILES)]
+        turned = [turn(A_BANK + u, hidden[u]) for u in range(SLOT_TILES)]
         result = keep.tile([P, ROW_TILES, C], F32, name="result")
         first = PIECES[0]
         results = [[result[:, q:q + 1, first] for q in range(ROW_TILES)]] + [[result[:, :, piece]] for piece in PIECES[1:]]
-        banks = [[A_BANK, A_BANK + 1], [Y_BANK], [B_BANK]]
+        banks = [LAST_B_BANKS[:2], LAST_B_BANKS[2:3], LAST_B_BANKS[3:4]]
         moving = []
         for piece in PIECES:
             count = piece.stop - piece.start

@@ -64,7 +64,10 @@ def tile_moe_two_glu_sigmoid_kernel(tc, xT, w1, w3, w2, gate, offs, dst, out):
 
         def load(matrix, s, rows=slice(0, PACK)):
             raw = stage.tile([P, rows.stop - rows.start, matrix.shape[1]], F32, name="raw", align_bytes=256)
-            nc.sync.dma_start(raw[:], matrix[s * K_PASS:(s + 1) * K_PASS, :].rearrange("(p j) w -> p j w", j=PACK)[:, rows, :])
+            if rows.stop - rows.start == PACK:
+                nc.sync.dma_start(raw[:].rearrange("p j w -> p (j w)"), matrix[s * K_PASS:(s + 1) * K_PASS, :].rearrange("(g r) w -> g (r w)", g=16))
+            else:
+                nc.sync.dma_start(raw[:], matrix[s * K_PASS:(s + 1) * K_PASS, :].rearrange("(p j) w -> p j w", j=PACK)[:, rows, :])
             return raw
 
         def values_tile(width):
@@ -243,9 +246,7 @@ def tile_moe_two_glu_sigmoid_kernel(tc, xT, w1, w3, w2, gate, offs, dst, out):
         for g, columns in enumerate(QUARTERS):
             quantize(quarters[g][:], weights[0][:, columns], weights[1][:, columns])
             product(b_groups[g][2][:, :P], slots_of(PASSES - 1, C, P), columns_of(weights, columns.start, P), False, True)
-            if g % 2:
-                pair = slice(columns.stop - 2 * P, columns.stop)
-                product(b_groups[-1][2][:, pair], slots_of(PASSES - 1, C + P, P), columns_of(weights, pair.start, 2 * P), False, columns.stop == H)
+        product(b_groups[-1][2][:], slots_of(PASSES - 1, C + P, P), columns_of(weights, 0, H), False, True)
 
         grouped = values_tile(N)
         weave(nc.scalar.copy, grouped[:], load(w2[1], 0)[:])

@@ -22,6 +22,7 @@ U16 = mybir.dt.uint16
 U8 = mybir.dt.uint8
 FP8X4 = mybir.dt.float8_e4m3fn_x4
 SIGMOID = mybir.ActivationFunctionType.Sigmoid
+COPY = mybir.ActivationFunctionType.Copy
 MULT = mybir.AluOpType.mult
 
 RUN = 2
@@ -266,10 +267,16 @@ def tile_moe_two_glu_sigmoid_kernel(tc, xT, w1, w3, w2, gate, offs, dst, out):
             woven = values_tile(count)[:]
             lay(woven, turned[piece.start // P][:, piece.start % P:piece.start % P + count])
             moving.append(quantized(woven, "hidden"))
-        for r in range(len(PIECES)):
+        for r in range(len(PIECES) - 1):
             second_layer(results[r], second, moving[r], banks[r])
-        for piece in PIECES:
-            for q in range(ROW_TILES):
-                scatter(1, piece, q, result[:, q, piece], gate_sb)
+            scatter(1, PIECES[r], 0, result[:, 0, PIECES[r]], gate_sb)
+        last = PIECES[-1]
+        sums = [bank(b, "y") for b in (LAST_B_BANKS[3], Y_BANK)]
+        for q in range(ROW_TILES):
+            product(sums[q][:, :P], second[q], columns_of(moving[-1], 0, P), True, True)
+        nc.vector.tensor_tensor(result[:, 0, last], sums[0][:, :P], gate_sb[:, C + last.start:C + last.stop], MULT)
+        nc.scalar.copy(result[:, 1, last], sums[1][:, :P])
+        nc.scalar.activation(placed[0][:].indirect(dst_sb[:, (C + last.start) // LIST:]), result[:, 0, last], COPY)
+        scatter(1, slice(0, C), 1, result[:, 1], gate_sb)
         for q in range(ROW_TILES):
             nc.sync.dma_start(out[q * P:(q + 1) * P, :], placed[q][:])

@@ -157,15 +157,6 @@ def tile_moe_two_glu_sigmoid_kernel(tc, xT, w1, w3, w2, gate, offs, dst, out):
         def lay(woven, turned):
             nc.scalar.copy(woven.bitcast(F32).rearrange("p (c w) -> p c w", w=2), turned)
 
-        def second_layer(results, second, moving, banks):
-            count = results[0].shape[2]
-            sums = [bank(b, "y") for b in banks]
-            for q in range(ROW_TILES):
-                product(sums[q % len(sums)][:, q * count:(q + 1) * count], second[q], columns_of(moving, 0, count), True, True)
-            share = ROW_TILES // len(sums)
-            for g, y in enumerate(sums):
-                nc.scalar.copy(results[g], y[:, :ROW_TILES * count].rearrange("p (q c) -> p q c", q=ROW_TILES)[:, g * share:(g + 1) * share])
-
         def scatter(e, piece, q, values, gate_sb):
             first, end = e * C + piece.start, e * C + piece.stop
             nc.vector.tensor_tensor(placed[q][:].indirect(dst_sb[:, first // LIST:end // LIST]), values, gate_sb[:, first:end], MULT)
@@ -249,34 +240,59 @@ def tile_moe_two_glu_sigmoid_kernel(tc, xT, w1, w3, w2, gate, offs, dst, out):
             product(b_groups[g][2][:, :P], slots_of(PASSES - 1, C, P), columns_of(weights, columns.start, P), False, True)
         product(b_groups[-1][2][:], slots_of(PASSES - 1, C + P, P), columns_of(weights, 0, H), False, True)
 
-        grouped = values_tile(N)
-        weave(nc.scalar.copy, grouped[:], load(w2[1], 0)[:])
+        raw = load(w2[1], 0)
+        grouped = [values_tile(P) for q in range(ROW_TILES)]
+        for q in range(ROW_TILES):
+            weave(nc.scalar.copy, grouped[q][:], raw[:, :, q * P:(q + 1) * P])
         hidden = [keep.tile([P, 2, P, 2], BF16, name=f"hidden{u}") for u in range(SLOT_TILES)]
         for u, columns, acc in b_groups:
             nc.vector.tensor_tensor(hidden[u][:].rearrange("s w p r -> s (w p r)")[:, columns], acc[:, :columns.stop - columns.start], sig[:, u, columns], MULT)
-        weights = quantized(grouped[:], "second")
-        second = [columns_of(weights, q * P, P) for q in range(ROW_TILES)]
+        second = {}
         turned = [turn(A_BANK + u, hidden[u]) for u in range(SLOT_TILES)]
         result = keep.tile([P, ROW_TILES, C], F32, name="result")
-        first = PIECES[0]
-        results = [[result[:, q:q + 1, first] for q in range(ROW_TILES)]] + [[result[:, :, piece]] for piece in PIECES[1:]]
-        banks = [LAST_B_BANKS[:2], LAST_B_BANKS[2:3], LAST_B_BANKS[3:4]]
         moving = []
         for piece in PIECES:
             count = piece.stop - piece.start
             woven = values_tile(count)[:]
             lay(woven, turned[piece.start // P][:, piece.start % P:piece.start % P + count])
-            moving.append(quantized(woven, "hidden"))
-        for r in range(len(PIECES) - 1):
-            second_layer(results[r], second, moving[r], banks[r])
-            scatter(1, PIECES[r], 0, result[:, 0, PIECES[r]], gate_sb)
-        last = PIECES[-1]
-        sums = [bank(b, "y") for b in (LAST_B_BANKS[3], Y_BANK)]
-        for q in range(ROW_TILES):
-            product(sums[q][:, :P], second[q], columns_of(moving[-1], 0, P), True, True)
-        nc.vector.tensor_tensor(result[:, 0, last], sums[0][:, :P], gate_sb[:, C + last.start:C + last.stop], MULT)
-        nc.scalar.copy(result[:, 1, last], sums[1][:, :P])
-        nc.scalar.activation(placed[0][:].indirect(dst_sb[:, (C + last.start) // LIST:]), result[:, 0, last], COPY)
-        scatter(1, slice(0, C), 1, result[:, 1], gate_sb)
-        for q in range(ROW_TILES):
-            nc.sync.dma_start(out[q * P:(q + 1) * P, :], placed[q][:])
+            moving.append(woven)
+        codes = {}
+
+        def sums(b, q, pieces):
+            if q not in second:
+                second[q] = columns_of(quantized(grouped[q][:], "second"), 0, P)
+            y = bank(b, "y")
+            first = PIECES[pieces[0]].start
+            for r in pieces:
+                piece = PIECES[r]
+                if r not in codes:
+                    codes[r] = quantized(moving[r], "hidden")
+                product(y[:, piece.start - first:piece.stop - first], second[q], columns_of(codes[r], 0, piece.stop - piece.start), True, True)
+            run = slice(first, PIECES[pieces[-1]].stop)
+            return y[:, :run.stop - run.start], q, run
+
+        def gated(y, q, run):
+            nc.vector.tensor_tensor(result[:, q, run], y, gate_sb[:, C + run.start:C + run.stop], MULT)
+
+        def plain(y, q, run):
+            nc.scalar.copy(result[:, q, run], y)
+
+        def place(q, first, end):
+            nc.scalar.activation(placed[q][:].indirect(dst_sb[:, (C + first) // LIST:(C + end) // LIST]), result[:, q, first:end], COPY)
+
+        def place_v(q, first, end):
+            nc.vector.tensor_copy(placed[q][:].indirect(dst_sb[:, (C + first) // LIST:(C + end) // LIST]), result[:, q, first:end])
+
+        def place_gated(q, first, end):
+            scatter(1, slice(first, end), q, result[:, q, first:end], gate_sb)
+
+        gated(*sums(2, 0, [0, 1]))
+        plain(*sums(3, 1, [0, 1]))
+        place(0, 0, 128)
+        gated(*sums(4, 0, [2]))
+        place_gated(1, 0, 128)
+        plain(*sums(5, 1, [2]))
+        place(0, 128, 256)
+        place_gated(1, 128, 256)
+        for q, queue in enumerate((nc.scalar, nc.sync)):
+            queue.dma_start(out[q * P:(q + 1) * P, :], placed[q][:])

@@ -29,7 +29,7 @@ RUN = 2
 
 VECTOR_COLUMNS = {("x", 0): 64, ("w1", 0): 192, ("w3", 0): 256, ("w2", 0): 64}
 W1_SHARES = (240, 176, 176, 176, 176)
-W3_SHARES = (224, 256, 288, 304)
+W3_SHARES = (224, 256, 288)
 
 PIECES = (slice(0, 64), slice(64, 128), slice(128, 256))
 
@@ -221,7 +221,20 @@ def tile_moe_two_glu_sigmoid_kernel(tc, xT, w1, w3, w2, gate, offs, dst, out):
         b_groups = [(0, columns, bank(b, "b")) for columns, b in zip(QUARTERS, LAST_B_BANKS)] + [(1, ALL, bank(LAST_B_BANKS[-1], "b"))]
         for s in range(PASSES - 1):
             raw = load(w3[1], s)
-            first_layer_pass(interleave_by_pair(raw, W3_SHARES[s]), 1, s, b_groups)
+            if s < PASSES - 2:
+                first_layer_pass(interleave_by_pair(raw, W3_SHARES[s]), 1, s, b_groups)
+            else:
+                weights = packed(H, "weight")
+                source = raw[:].rearrange("k j (half p w r) -> k half p w j r", half=2, w=2, r=2)
+                for half, copy in enumerate((nc.vector.tensor_copy, nc.scalar.copy)):
+                    grouped = values_tile(H // 2)
+                    copy(grouped[:].rearrange("k (w p r j) -> k p w j r", w=2, r=2, j=PACK), source[:, half])
+                    for w in range(2):
+                        columns = QUARTERS[2 * w + half]
+                        quantize(grouped[:, w * P * PACK:(w + 1) * P * PACK], weights[0][:, columns], weights[1][:, columns])
+                for u, columns, acc in b_groups:
+                    count = columns.stop - columns.start
+                    product(acc[:, :count], slots_of(s, C + u * P, P), columns_of(weights, columns.start, count), False, False)
             if s == 1:
                 sig = raw[:, :SLOT_TILES]
                 sigmoids(sig.rearrange("s u (w p r) -> s u w p r", w=2, r=2), a_groups)

@@ -25,9 +25,10 @@ SIGMOID = mybir.ActivationFunctionType.Sigmoid
 COPY = mybir.ActivationFunctionType.Copy
 MULT = mybir.AluOpType.mult
 
+WINDOW = 768
 RUN = 2
 
-VECTOR_COLUMNS = {("x", 0): 64, ("w1", 0): 192, ("w3", 0): 256, ("w2", 0): 64}
+VECTOR_COLUMNS = {("x", 0): 0, ("w1", 0): 192, ("w3", 0): 256, ("w2", 0): 144}
 W1_SHARES = (240, 176, 176, 176, 176)
 W3_SHARES = (224, 256, 288)
 
@@ -53,13 +54,15 @@ def tile_moe_two_glu_sigmoid_kernel(tc, xT, w1, w3, w2, gate, offs, dst, out):
         dst_sb = lists.tile([P, E * C // LIST], U16, name="dst_sb")
 
         scale_tiles = (PASSES + PLANES - 1) // PLANES
-        token_scales = [keep.tile([P, T], U8, name=f"token_scales{g}", align_bytes=64) for g in range(scale_tiles)]
+        token_scales = [keep.tile([P, WINDOW], U8, name=f"token_scales{g}", align_bytes=64) for g in range(scale_tiles)]
         slot_scales = [keep.tile([P, E * C], U8, name=f"slot_scales{g}", align_bytes=64) for g in range(scale_tiles)]
         for plane in token_scales:
             nc.gpsimd.memset(plane[:], 0)
         identity = keep.tile([P, P], F32, name="identity")
         make_identity(nc, identity[:])
-        token_words = [keep.tile([P, T], U32, name=f"token_words{s}", align_bytes=64) for s in range(PASSES)]
+        all_words = keep.tile([P, (PASSES - 1) * T + WINDOW], U32, name="token_words", align_bytes=64)
+        nc.gpsimd.memset(all_words[:, PASSES * T:], 0)
+        token_words = [all_words[:, (PASSES - 1 - s) * T:(PASSES - 1 - s) * T + WINDOW] for s in range(PASSES)]
         slot_words = [keep.tile([P, E * C], U32, name=f"slot_words{s}", align_bytes=64) for s in range(PASSES)]
         placed = [keep.tile([P, T], F32, name=f"placed{q}", align_bytes=256) for q in range(ROW_TILES)]
 
@@ -80,7 +83,8 @@ def tile_moe_two_glu_sigmoid_kernel(tc, xT, w1, w3, w2, gate, offs, dst, out):
         def interleave(raw, cut):
             width = raw.shape[2]
             grouped = values_tile(width)
-            weave(nc.vector.tensor_copy, grouped[:, :cut * PACK], raw[:, :, :cut])
+            if cut:
+                weave(nc.vector.tensor_copy, grouped[:, :cut * PACK], raw[:, :, :cut])
             weave(nc.scalar.copy, grouped[:, cut * PACK:], raw[:, :, cut:])
             return grouped
 
@@ -100,8 +104,8 @@ def tile_moe_two_glu_sigmoid_kernel(tc, xT, w1, w3, w2, gate, offs, dst, out):
         def bank(b, name):
             return psum.tile([P, 512], F32, tag=f"bank{b}", name=name)
 
-        def gather(slots, tokens, e):
-            nc.vector.tensor_copy(slots[:, e * C:(e + 1) * C], tokens[:].indirect(offs_sb[:, e * C // LIST:(e + 1) * C // LIST]))
+        def gather(slots, window):
+            nc.vector.tensor_copy(slots[:], window.indirect(offs_sb[:]))
 
         def product(acc, stationary, moving, start, stop):
             nc.tensor.matmul_mx(
@@ -182,11 +186,10 @@ def tile_moe_two_glu_sigmoid_kernel(tc, xT, w1, w3, w2, gate, offs, dst, out):
                 nc.sync.dma_start(offs_sb[:], offs)
                 gate_sb = spread_gate()
             grouped = interleave(raw, VECTOR_COLUMNS["x", 0])
-            quantize(grouped[:], token_words[s][:], token_scales[s // PLANES][4 * (s % PLANES):P, :])
-            for e in range(E):
-                gather(slot_words[s], token_words[s], e)
-                if s % PLANES == PLANES - 1 or s == PASSES - 1:
-                    gather(slot_scales[s // PLANES], token_scales[s // PLANES], e)
+            quantize(grouped[:], token_words[s][:, :T], token_scales[s // PLANES][4 * (s % PLANES):P, :T])
+            gather(slot_words[s], token_words[s])
+            if s % PLANES == PLANES - 1 or s == PASSES - 1:
+                gather(slot_scales[s // PLANES], token_scales[s // PLANES][:])
 
         a_groups = whole_groups(A_BANK, "a")
         for s in range(PASSES):

@@ -26,7 +26,7 @@ COPY = mybir.ActivationFunctionType.Copy
 MULT = mybir.AluOpType.mult
 
 WINDOW = 768
-RUN = 2
+RUN = 4
 
 VECTOR_COLUMNS = {("x", 0): 0, ("w1", 0): 192, ("w3", 0): 256, ("w2", 0): 144}
 W1_SHARES = (240, 176, 176, 176, 176)
@@ -132,8 +132,8 @@ def tile_moe_two_glu_sigmoid_kernel(tc, xT, w1, w3, w2, gate, offs, dst, out):
 
         def interleave_by_pair(raw, cut):
             grouped = values_tile(H)
-            to = grouped[:].rearrange("k (w p r j) -> k p w j r", w=2, r=2, j=PACK)
-            source = raw[:].rearrange("k j (p w r) -> k p w j r", w=2, r=2)
+            to = grouped[:].rearrange("k (w p r j) -> k p j w r", w=2, r=2, j=PACK)
+            source = raw[:].rearrange("k j (p w r) -> k p j w r", w=2, r=2)
             nc.vector.tensor_copy(to[:, :cut // PACK], source[:, :cut // PACK])
             nc.scalar.copy(to[:, cut // PACK:], source[:, cut // PACK:])
             return grouped
@@ -228,10 +228,10 @@ def tile_moe_two_glu_sigmoid_kernel(tc, xT, w1, w3, w2, gate, offs, dst, out):
                 first_layer_pass(interleave_by_pair(raw, W3_SHARES[s]), 1, s, b_groups)
             else:
                 weights = packed(H, "weight")
-                source = raw[:].rearrange("k j (half p w r) -> k half p w j r", half=2, w=2, r=2)
+                source = raw[:].rearrange("k j (half p w r) -> k half p j w r", half=2, w=2, r=2)
                 for half, copy in enumerate((nc.vector.tensor_copy, nc.scalar.copy)):
                     grouped = values_tile(H // 2)
-                    copy(grouped[:].rearrange("k (w p r j) -> k p w j r", w=2, r=2, j=PACK), source[:, half])
+                    copy(grouped[:].rearrange("k (w p r j) -> k p j w r", w=2, r=2, j=PACK), source[:, half])
                     for w in range(2):
                         columns = QUARTERS[2 * w + half]
                         quantize(grouped[:, w * P * PACK:(w + 1) * P * PACK], weights[0][:, columns], weights[1][:, columns])

from contextlib import ExitStack

import concourse.mybir as mybir
from concourse.masks import make_identity

K, T, E, C, H, N = 2560, 512, 2, 256, 512, 256
P = 128
PACK = 4
K_PASS = P * PACK
PASSES = K // K_PASS
PLANES = 4
BLOCK = 32
LIST = 16
SLOT_TILES = C // P
ROW_TILES = N // P
FLOPS = 2 * E * C * (2 * K * H + H * N)

F32 = mybir.dt.float32
BF16 = mybir.dt.bfloat16
U32 = mybir.dt.uint32
U16 = mybir.dt.uint16
U8 = mybir.dt.uint8
FP8X4 = mybir.dt.float8_e4m3fn_x4
SIGMOID = mybir.ActivationFunctionType.Sigmoid
COPY = mybir.ActivationFunctionType.Copy
MULT = mybir.AluOpType.mult

WINDOW = 768
RUN = 4

VECTOR_COLUMNS = {("x", 0): 0, ("w1", 0): 192, ("w3", 0): 256, ("w2", 0): 144}
W1_SHARES = (240, 176, 176, 176, 176)
W3_SHARES = (224, 256, 288)

PIECES = (slice(0, 64), slice(64, 128), slice(128, 256))

ALL = slice(0, H)
QUARTERS = [slice(g * P, (g + 1) * P) for g in range(H // P)]

A_BANK, B_BANK, Y_BANK, TURN_BANK = 0, 2, 5, 6
LAST_B_BANKS = (2, 3, 4, 6, 7)


def tile_moe_two_glu_sigmoid_kernel(tc, xT, w1, w3, w2, gate, offs, dst, out):
    nc = tc.nc
    with ExitStack() as ctx:
        lists = ctx.enter_context(tc.tile_pool(name="lists", bufs=1))
        keep = ctx.enter_context(tc.tile_pool(name="keep", bufs=1))
        stage = ctx.enter_context(tc.tile_pool(name="stage", bufs=8))
        work = ctx.enter_context(tc.tile_pool(name="work", bufs=4))
        psum = ctx.enter_context(tc.psum_pool(name="psum", bufs=1))

        offs_sb = lists.tile([P, E * C // LIST], U16, name="offs_sb")
        dst_sb = lists.tile([P, E * C // LIST], U16, name="dst_sb")

        scale_tiles = (PASSES + PLANES - 1) // PLANES
        token_scales = [keep.tile([P, WINDOW], U8, name=f"token_scales{g}", align_bytes=64) for g in range(scale_tiles)]
        slot_scales = [keep.tile([P, E * C], U8, name=f"slot_scales{g}", align_bytes=64) for g in range(scale_tiles)]
        for plane in token_scales:
            nc.gpsimd.memset(plane[:], 0)
        identity = keep.tile([P, P], F32, name="identity")
        make_identity(nc, identity[:])
        all_words = keep.tile([P, (PASSES - 1) * T + WINDOW], U32, name="token_words", align_bytes=64)
        nc.gpsimd.memset(all_words[:, PASSES * T:], 0)
        token_words = [all_words[:, (PASSES - 1 - s) * T:(PASSES - 1 - s) * T + WINDOW] for s in range(PASSES)]
        slot_words = [keep.tile([P, E * C], U32, name=f"slot_words{s}", align_bytes=64) for s in range(PASSES)]
        placed = [keep.tile([P, T], F32, name=f"placed{q}", align_bytes=256) for q in range(ROW_TILES)]

        def load(matrix, s, rows=slice(0, PACK)):
            raw = stage.tile([P, rows.stop - rows.start, matrix.shape[1]], F32, name="raw", align_bytes=256)
            if rows.stop - rows.start == PACK:
                nc.sync.dma_start(raw[:].rearrange("p j w -> p (j w)"), matrix[s * K_PASS:(s + 1) * K_PASS, :].rearrange("(g r) w -> g (r w)", g=16))
            else:
                nc.sync.dma_start(raw[:], matrix[s * K_PASS:(s + 1) * K_PASS, :].rearrange("(p j) w -> p j w", j=PACK)[:, rows, :])
            return raw

        def values_tile(width):
            return work.tile([P, width * PACK], BF16, name=f"grouped{width}", align_bytes=64)

        def weave(copy, grouped, raw):
            copy(grouped.rearrange("p (c i j) -> p c j i", i=RUN, j=PACK), raw.rearrange("p j (c i) -> p c j i", i=RUN))

        def interleave(raw, cut):
            width = raw.shape[2]
            grouped = values_tile(width)
            if cut:
                weave(nc.vector.tensor_copy, grouped[:, :cut * PACK], raw[:, :, :cut])
            weave(nc.scalar.copy, grouped[:, cut * PACK:], raw[:, :, cut:])
            return grouped

        def quantize(values, codes, scales):
            nc.vector.quantize_mx(out=codes.bitcast(FP8X4), scales=scales, in_=values)

        def packed(width, name):
            codes = work.tile([P, width], U32, name=f"{name}_codes", align_bytes=64)
            scales = work.tile([P, width], U8, name=f"{name}_scales", align_bytes=64)
            return codes, scales

        def quantized(values, name):
            codes, scales = packed(values.shape[1] // PACK, name)
            quantize(values, codes[:], scales[:])
            return codes, scales

        def bank(b, name):
            return psum.tile([P, 512], F32, tag=f"bank{b}", name=name)

        def gather(slots, window):
            nc.vector.tensor_copy(slots[:], window.indirect(offs_sb[:]))

        def product(acc, stationary, moving, start, stop):
            nc.tensor.matmul_mx(
                out=acc,
                lhsT=stationary[0].bitcast(FP8X4),
                lhsT_scale=stationary[1],
                rhs=moving[0].bitcast(FP8X4),
                rhs_scale=moving[1],
                start=start,
                stop=stop,
            )

        def columns_of(operand, first, count):
            return [part[:, first:first + count] for part in operand]

        def slots_of(s, first, count):
            return columns_of((slot_words[s], slot_scales[s // PLANES][4 * (s % PLANES):P]), first, count)

        def first_layer_pass(grouped, e, s, groups):
            weights = quantized(grouped[:], "weight")
            for u, columns, acc in groups:
                count = columns.stop - columns.start
                product(acc[:, :count], slots_of(s, e * C + u * P, P), columns_of(weights, columns.start, count), s == 0, s == PASSES - 1)

        def interleave_by_pair(raw, cut):
            grouped = values_tile(H)
            to = grouped[:].rearrange("k (w p r j) -> k p j w r", w=2, r=2, j=PACK)
            source = raw[:].rearrange("k j (p w r) -> k p j w r", w=2, r=2)
            nc.vector.tensor_copy(to[:, :cut // PACK], source[:, :cut // PACK])
            nc.scalar.copy(to[:, cut // PACK:], source[:, cut // PACK:])
            return grouped

        def by_pair(columns):
            return columns.rearrange("s (p w r) -> s w p r", w=2, r=2)

        def sigmoids(sig, groups):
            for u, columns, acc in groups:
                nc.scalar.activation(sig[:, u], by_pair(acc[:]), SIGMOID)

        def hidden_pairs(groups, sig):
            hidden = [keep.tile([P, 2, P, 2], BF16, name=f"hidden{u}") for u in range(SLOT_TILES)]
            for u, columns, acc in groups:
                nc.vector.tensor_tensor(hidden[u][:], by_pair(acc[:]), sig[:, u], MULT)
            return hidden

        def turn(b, hidden):
            pairs = hidden[:].rearrange("s w p r -> s (w p r)").bitcast(F32)
            turned = bank(b, "turned")
            for w in range(2):
                nc.tensor.transpose(turned[:, w * P:(w + 1) * P], pairs[:, w * P:(w + 1) * P], identity[:])
            return turned[:, :2 * P].rearrange("p (w c) -> p c w", w=2)

        def lay(woven, turned):
            nc.scalar.copy(woven.bitcast(F32).rearrange("p (c w) -> p c w", w=2), turned)

        def scatter(e, piece, q, values, gate_sb):
            first, end = e * C + piece.start, e * C + piece.stop
            nc.vector.tensor_tensor(placed[q][:].indirect(dst_sb[:, first // LIST:end // LIST]), values, gate_sb[:, first:end], MULT)

        def spread_gate():
            runs = E * C // BLOCK
            cut = keep.tile([P, BLOCK], F32, name="gate_cut", align_bytes=256)
            nc.scalar.dma_start(cut[:], gate[:P // runs, :].rearrange("r (g b) -> (r g) b", b=BLOCK))
            upright = keep.tile([P, BLOCK], F32, name="gate_upright", align_bytes=64)
            nc.vector.transpose(upright[:], cut[:])
            repeated = keep.tile([P, runs, BLOCK], F32, name="gate_repeated", align_bytes=64)
            nc.vector.tensor_copy(repeated[:], upright[:, :runs].unsqueeze(2).to_broadcast([P, runs, BLOCK]))
            gate_sb = keep.tile([P, E * C], F32, name="gate_sb", align_bytes=64)
            nc.vector.transpose(gate_sb[:], repeated[:].rearrange("p g b -> p (g b)"))
            return gate_sb

        def whole_groups(first_bank, name):
            return [(u, ALL, bank(first_bank + u, f"{name}{u}")) for u in range(SLOT_TILES)]

        for s in range(PASSES):
            raw = load(xT, s)
            if s == 0:
                nc.sync.dma_start(offs_sb[:], offs)
                gate_sb = spread_gate()
            grouped = interleave(raw, VECTOR_COLUMNS["x", 0])
            quantize(grouped[:], token_words[s][:, :T], token_scales[s // PLANES][4 * (s % PLANES):P, :T])
            gather(slot_words[s], token_words[s])
            if s % PLANES == PLANES - 1 or s == PASSES - 1:
                gather(slot_scales[s // PLANES], token_scales[s // PLANES][:])

        a_groups = whole_groups(A_BANK, "a")
        for s in range(PASSES):
            first_layer_pass(interleave(load(w1[0], s), VECTOR_COLUMNS["w1", 0]), 0, s, a_groups)
        sig = keep.tile([P, SLOT_TILES, 2, P, 2], F32, name="sig0", align_bytes=64)
        sigmoids(sig, a_groups)
        b_groups = whole_groups(B_BANK, "b")
        for s in range(PASSES):
            first_layer_pass(interleave(load(w3[0], s), VECTOR_COLUMNS["w3", 0]), 0, s, b_groups)
        weights = quantized(interleave(load(w2[0], 0), VECTOR_COLUMNS["w2", 0])[:], "second")
        second = [columns_of(weights, q * P, P) for q in range(ROW_TILES)]
        nc.sync.dma_start(dst_sb[:], dst)
        hidden = hidden_pairs(b_groups, sig)

        a_groups = whole_groups(A_BANK, "a")
        y = bank(Y_BANK, "y")
        for s in range(PASSES):
            raw = load(w1[1], s)
            first_layer_pass(interleave(raw, W1_SHARES[s]), 1, s, a_groups)
            if s == 0:
                woven = raw[:, 0].bitcast(BF16)
                for u in range(SLOT_TILES):
                    lay(woven[:, u * P * PACK:(u + 1) * P * PACK], turn(TURN_BANK + u, hidden[u]))
                moving = quantized(woven, "hidden")
                for q in range(ROW_TILES):
                    product(y[:, q * C:(q + 1) * C], second[q], columns_of(moving, 0, C), True, True)
            else:
                u, q = divmod(s - 1, ROW_TILES)
                nc.scalar.copy(raw[:, 0, :P], y[:, q * C + u * P:q * C + (u + 1) * P])
                scatter(0, slice(u * P, (u + 1) * P), q, raw[:, 0, :P], gate_sb)

        b_groups = [(0, columns, bank(b, "b")) for columns, b in zip(QUARTERS, LAST_B_BANKS)] + [(1, ALL, bank(LAST_B_BANKS[-1], "b"))]
        for s in range(PASSES - 1):
            raw = load(w3[1], s)
            if s < PASSES - 2:
                first_layer_pass(interleave_by_pair(raw, W3_SHARES[s]), 1, s, b_groups)
            else:
                weights = packed(H, "weight")
                source = raw[:].rearrange("k j (half p w r) -> k half p j w r", half=2, w=2, r=2)
                for half, copy in enumerate((nc.vector.tensor_copy, nc.scalar.copy)):
                    grouped = values_tile(H // 2)
                    copy(grouped[:].rearrange("k (w p r j) -> k p j w r", w=2, r=2, j=PACK), source[:, half])
                    for w in range(2):
                        columns = QUARTERS[2 * w + half]
                        quantize(grouped[:, w * P * PACK:(w + 1) * P * PACK], weights[0][:, columns], weights[1][:, columns])
                for u, columns, acc in b_groups:
                    count = columns.stop - columns.start
                    product(acc[:, :count], slots_of(s, C + u * P, P), columns_of(weights, columns.start, count), False, False)
            if s == 1:
                sig = raw[:, :SLOT_TILES]
                sigmoids(sig.rearrange("s u (w p r) -> s u w p r", w=2, r=2), a_groups)

        quarters = [values_tile(P) for columns in QUARTERS]
        for v in range(2):
            rows = slice(2 * v, 2 * v + 2)
            source = load(w3[1], PASSES - 1, rows)[:].rearrange("k j (half p w r) -> k w half p j r", half=2, w=2, r=2)
            for g, grouped in enumerate(quarters):
                w, half = divmod(g, 2)
                copy = nc.vector.tensor_copy if w != v else nc.scalar.copy
                copy(grouped[:].rearrange("k (p r j) -> k p j r", r=2, j=PACK)[:, :, rows], source[:, w, half])
        weights = packed(H, "weight")
        for g, columns in enumerate(QUARTERS):
            quantize(quarters[g][:], weights[0][:, columns], weights[1][:, columns])
            product(b_groups[g][2][:, :P], slots_of(PASSES - 1, C, P), columns_of(weights, columns.start, P), False, True)
        product(b_groups[-1][2][:], slots_of(PASSES - 1, C + P, P), columns_of(weights, 0, H), False, True)

        raw = load(w2[1], 0)
        grouped = [values_tile(P) for q in range(ROW_TILES)]
        for q in range(ROW_TILES):
            weave(nc.scalar.copy, grouped[q][:], raw[:, :, q * P:(q + 1) * P])
        hidden = [keep.tile([P, 2, P, 2], BF16, name=f"hidden{u}") for u in range(SLOT_TILES)]
        for u, columns, acc in b_groups:
            nc.vector.tensor_tensor(hidden[u][:].rearrange("s w p r -> s (w p r)")[:, columns], acc[:, :columns.stop - columns.start], sig[:, u, columns], MULT)
        second = {}
        turned = [turn(A_BANK + u, hidden[u]) for u in range(SLOT_TILES)]
        result = keep.tile([P, ROW_TILES, C], F32, name="result")
        moving = []
        for piece in PIECES:
            count = piece.stop - piece.start
            woven = values_tile(count)[:]
            lay(woven, turned[piece.start // P][:, piece.start % P:piece.start % P + count])
            moving.append(woven)
        codes = {}

        def sums(b, q, pieces):
            if q not in second:
                second[q] = columns_of(quantized(grouped[q][:], "second"), 0, P)
            y = bank(b, "y")
            first = PIECES[pieces[0]].start
            for r in pieces:
                piece = PIECES[r]
                if r not in codes:
                    codes[r] = quantized(moving[r], "hidden")
                product(y[:, piece.start - first:piece.stop - first], second[q], columns_of(codes[r], 0, piece.stop - piece.start), True, True)
            run = slice(first, PIECES[pieces[-1]].stop)
            return y[:, :run.stop - run.start], q, run

        def gated(y, q, run):
            nc.vector.tensor_tensor(result[:, q, run], y, gate_sb[:, C + run.start:C + run.stop], MULT)

        def plain(y, q, run):
            nc.scalar.copy(result[:, q, run], y)

        def place(q, first, end):
            nc.scalar.activation(placed[q][:].indirect(dst_sb[:, (C + first) // LIST:(C + end) // LIST]), result[:, q, first:end], COPY)

        def place_v(q, first, end):
            nc.vector.tensor_copy(placed[q][:].indirect(dst_sb[:, (C + first) // LIST:(C + end) // LIST]), result[:, q, first:end])

        def place_gated(q, first, end):
            scatter(1, slice(first, end), q, result[:, q, first:end], gate_sb)

        gated(*sums(2, 0, [0, 1]))
        plain(*sums(3, 1, [0, 1]))
        place(0, 0, 128)
        gated(*sums(4, 0, [2]))
        place_gated(1, 0, 128)
        plain(*sums(5, 1, [2]))
        place(0, 128, 256)
        place_gated(1, 128, 256)
        for q, queue in enumerate((nc.scalar, nc.sync)):
            queue.dma_start(out[q * P:(q + 1) * P, :], placed[q][:])
